import numpy as np
import ml_dtypes


def mxq(x, axis, fmt="e4m3"):
    dtype, down = {"e4m3": (ml_dtypes.float8_e4m3fn, 7), "e5m2": (ml_dtypes.float8_e5m2, 14)}[fmt]
    v = np.moveaxis(np.asarray(x, np.float32).astype(ml_dtypes.bfloat16).astype(np.float64), axis, -1)
    blocks = v.reshape(v.shape[:-1] + (-1, 32))
    amax = np.abs(blocks).max(-1, keepdims=True)
    byte = np.maximum(np.where(amax > 0, np.frexp(amax)[1] - 1 + 127, 0) - down, 1)
    scale = np.exp2(byte - 127.0)
    codes = (blocks / scale).astype(np.float32).astype(dtype).astype(np.float64)
    return np.moveaxis((codes * scale).reshape(v.shape), -1, axis)


WIDE = False


def mx_kscale(k):
    if not WIDE:
        return np.ones(k)
    levels = np.array([10, -10, 5, -5, 0])
    if k % 512:
        return np.exp2(np.random.permutation(np.resize(levels, k // 32))).repeat(32)
    a = np.empty((k // 512, 16))
    for p in range(k // 512):
        a[p, :8] = np.random.permutation(np.resize(levels, 8))
        for g in range(8):
            far = levels[np.abs(levels - a[p, g]) >= 10]
            a[p, g + 8] = far[np.random.randint(len(far))]
    return np.exp2(a.ravel()).repeat(32)


def f64(x):
    return np.asarray(x).astype(np.float64)


def striped(idx):
    return np.tile(idx.reshape(-1, 16).T, (8, 1)).astype(np.uint16)


def unstriped(offs):
    return offs[:16].T.reshape(-1).astype(np.int64)


E2M1 = np.array([0.0, 0.5, 1.0, 1.5, 2.0, 3.0, 4.0, 6.0, -0.0, -0.5, -1.0, -1.5, -2.0, -3.0, -4.0, -6.0])


def pack_weight(w, fmt):
    k, n = w.shape
    w = f64(np.asarray(w, np.float32).astype(ml_dtypes.bfloat16)).reshape(k // 32, 32, n)
    amax = np.abs(w).max(1)
    if fmt == "e4m3":
        byte = np.frexp(amax)[1] - 1 + 127 - 7
    else:
        mant, ex = np.frexp(amax / 6.0)
        byte = np.where(mant > 0.5, ex, ex - 1) + 127
    byte = np.clip(np.where(amax > 0, byte, 1), 1, 254)
    scaled = (w * np.exp2(127.0 - byte)[:, None, :]).reshape(k, n).astype(np.float32)
    by_word = np.ascontiguousarray(scaled.reshape(k // 512, 128, 4, n).transpose(0, 1, 3, 2))
    if fmt == "e4m3":
        words = by_word.astype(ml_dtypes.float8_e4m3fn).view(np.uint8)
    else:
        c = by_word.astype(ml_dtypes.float4_e2m1fn).view(np.uint8) & 0xF
        words = (c[..., 0::2] | (c[..., 1::2] << 4)).reshape(k // 512, 128, 2 * n)
    return np.ascontiguousarray(words), np.ascontiguousarray(byte.astype(np.uint8).reshape(k // 512, 16, n))


def unpack_weight(words, scales, fmt):
    g, _, n = scales.shape
    words = np.ascontiguousarray(words).reshape(g, 128, n, -1)
    if fmt == "e4m3":
        vals = words.view(ml_dtypes.float8_e4m3fn).astype(np.float64)
    else:
        nib = np.empty((g, 128, n, 4), np.uint8)
        nib[..., 0::2] = words & 0xF
        nib[..., 1::2] = words >> 4
        vals = E2M1[nib]
    vals = vals * np.repeat(np.exp2(scales.astype(np.float64) - 127.0), 8, axis=1)[..., None]
    return vals.transpose(0, 1, 3, 2).reshape(g * 512, n)


def gelu(v):
    return 0.5 * v * (1.0 + np.tanh(np.sqrt(2.0 / np.pi) * (v + 0.044715 * v**3)))


def striped8(idx):
    return np.concatenate([v.reshape(-1, 16).T for v in idx]).astype(np.uint16)


def unstriped8(offs):
    return np.stack([offs[16 * g:16 * g + 16].T.reshape(-1) for g in range(8)]).astype(np.int64)


def runs(v, idx8):
    k = np.arange(v.shape[0])
    return v[k[:, None], idx8[k % 512 // 64]]


def put_heads(h, wgs, idx8, t2):
    r = np.arange(h.shape[0])
    page = np.zeros((h.shape[0], t2))
    page[r[:, None], idx8[r % 512 // 64]] = wgs[r // 4 % 128] * h
    return page


def often(T, S):
    return np.random.permutation(T)[(T * np.random.uniform(0, 1, S) ** 4).astype(np.int64)]


K, H, N, T, S, T2 = 1024, 1024, 512, 2048, 1024, 2048

def setup_inputs():
    n = np.random.standard_normal
    s = mx_kscale(K)[:, None]
    u = mx_kscale(H)[:, None]
    tab_words, tab_scales = pack_weight(n((K, T)) * s, "e4m3")
    wa_words, wa_scales = pack_weight(n((K, H)) / np.sqrt(K) / s * u.T, "e2m1")
    wb = (n((K, H)) / np.sqrt(K) / s * u.T).astype(np.float32)
    wc = (n((H, N)) / np.sqrt(H) / u).astype(np.float32)
    low = (0.5 * n(N)).astype(np.float32)
    wgo = np.repeat(np.random.uniform(0.5, 2.0, (8, S)), 16, axis=0).astype(np.float32)
    offs = striped8(np.stack([often(T, S) for _ in range(8)]))
    offs2 = striped8(np.stack([np.random.permutation(T2)[:S] for _ in range(8)]))
    return {"tab_words": tab_words, "tab_scales": tab_scales, "offs": offs,
            "wa_words": wa_words, "wa_scales": wa_scales, "wb": wb, "wc": wc,
            "low": low, "wgo": wgo, "offs2": offs2}

def reference(tab_words, tab_scales, offs, wa_words, wa_scales, wb, wc, low, wgo, offs2):
    v = runs(unpack_weight(tab_words, tab_scales, "e4m3"), unstriped8(offs))
    a = unpack_weight(wa_words, wa_scales, "e2m1").T @ v
    b = mxq(f64(wb), 0, "e4m3").T @ v
    h = np.minimum(a, b)
    y = mxq(f64(wc), 0, "e4m3").T @ mxq(h, 0, "e4m3")
    y = np.maximum(y, f64(low)[:, None])
    out = put_heads(y, f64(wgo), unstriped8(offs2), T2)
    return out

@@ -1,0 +1,255 @@
+from contextlib import ExitStack
+
+import concourse.mybir as mybir
+
+K, H, N, T, S, T2 = 1024, 1024, 512, 2048, 1024, 2048
+FLOPS = 2 * (2 * K * H * S + H * N * S)
+
+F32 = mybir.dt.float32
+BF16 = mybir.dt.bfloat16
+I32 = mybir.dt.int32
+U32 = mybir.dt.uint32
+U16 = mybir.dt.uint16
+U8 = mybir.dt.uint8
+FP8X4 = mybir.dt.float8_e4m3fn_x4
+FP4X4 = mybir.dt.float4_e2m1fn_x4
+ALU = mybir.AluOpType
+
+P = 128
+UNIT = 128
+HALF = 512
+GROUPS = (128, 128, 256, 256, 256)
+SCATTERS = ((0,), (1,), (2,), (3, 4))
+WB_SCALAR_QUARTERS = (3, 3, 2, 2)
+WC_SCALAR_QUARTERS = (2, 2)
+
+
+def tile_list_blood_stock_offers_kernel(
+    tc, tab_words, tab_scales, offs, wa_words, wa_scales, wb, wc, low, wgo, offs2, out
+):
+    nc = tc.nc
+    with ExitStack() as ctx:
+        keep = ctx.enter_context(tc.tile_pool(name="keep", bufs=1))
+        ring = ctx.enter_context(tc.tile_pool(name="ring", bufs=2))
+        psum = ctx.enter_context(tc.psum_pool(name="psum", bufs=1))
+
+        def held(shape, dtype, name, tag=None):
+            return keep.tile(shape, dtype, name=name, tag=tag or name, align_bytes=64)
+
+        picks = keep.tile([P, S // 16], U16, name="picks")
+        nc.sync.dma_start(picks[:], offs)
+        slots = keep.tile([P, S // 16], U16, name="slots")
+        nc.sync.dma_start(slots[:], offs2)
+        scale_table = held([P, T], U8, "scale_table", tag="after_scale_gather")
+        nc.gpsimd.memset(scale_table[:].bitcast(I32), 0)
+        word_table = [held([P, T], U32, "word_table0", tag="after_word_gather"), held([P, T], U32, "word_table1")]
+
+        def load_words(a):
+            nc.sync.dma_start(
+                word_table[a][:].bitcast(I32), tab_words[a].rearrange("p n t -> p (n t)").bitcast(I32)
+            )
+
+        load_words(0)
+        for a in range(2):
+            nc.sync.dma_start(scale_table[a:P:8, :].bitcast(I32), tab_scales[a].bitcast(I32))
+        load_words(1)
+        wa_raw = held([P, 4096], U8, "wa_raw", tag="after_wa")
+        nc.sync.dma_start(
+            wa_raw[:].bitcast(I32).rearrange("p (a n) -> p a n", a=2),
+            wa_words.bitcast(I32).rearrange("a p n -> p a n"),
+        )
+        was_raw = held([P, 2048], U8, "was_raw")
+        nc.vector.memset(was_raw[:].bitcast(I32), 0)
+        v_scales = [held([P, S], U8, "v_scales%d" % a) for a in range(2)]
+        nc.vector.memset(v_scales[1][:].bitcast(I32), 0)
+        was_rows = wa_scales.bitcast(I32).rearrange("a (d r) n -> r d a n", r=4)
+        for r in range(4):
+            nc.sync.dma_start(
+                was_raw[r:P:32, :].bitcast(I32).rearrange("p (a n) -> p a n", a=2), was_rows[r]
+            )
+
+        def load_wb(dst, a, b):
+            nc.sync.dma_start(
+                dst, wb[512 * a : 512 * (a + 1), 512 * b : 512 * (b + 1)].rearrange("(p j) c -> p j c", j=4)
+            )
+
+        first_wb = held([P, 4, 512], F32, "first_wb")
+        load_wb(first_wb[:], 0, 0)
+
+        picked_scales = held([P, S], U8, "picked_scales", tag="after_moves")
+        nc.vector.tensor_copy(picked_scales[:], scale_table[:].indirect(picks[:]))
+        nc.vector.tensor_copy(v_scales[0][:].bitcast(I32), picked_scales[:].bitcast(I32))
+        for a, queue, rows in ((0, nc.sync, (1, 2, 3)), (1, nc.sync, (0, 1, 2, 3))):
+            for r in rows:
+                queue.dma_start(
+                    v_scales[a][r:P:32, :].bitcast(I32), picked_scales[8 * r + a : P : 32, :].bitcast(I32)
+                )
+        first_words = held([P, S], U32, "first_words", tag="after_scale_gather")
+        nc.vector.tensor_copy(first_words[:], word_table[0][:].indirect(picks[:]))
+        v_words = {(0, hf): first_words[:, HALF * hf : HALF * (hf + 1)] for hf in range(2)}
+        for hf in range(2):
+            second_words = held([P, HALF], U32, "second_words%d" % hf)
+            nc.vector.tensor_copy(second_words[:], word_table[1][:].indirect(picks[:, 32 * hf : 32 * (hf + 1)]))
+            v_words[1, hf] = second_words[:]
+
+        late = held([P, 3 * 2048], F32, "late", tag="after_word_gather")
+        wb_raw = {(0, 0): first_wb[:]}
+        for n, (a, b) in enumerate(((1, 0), (0, 1), (1, 1))):
+            wb_raw[a, b] = late[:, 2048 * n : 2048 * (n + 1)].rearrange("p (j c) -> p j c", j=4)
+            load_wb(wb_raw[a, b], a, b)
+
+        wa_codes = held([P, 4096], U8, "wa_codes")
+        nc.vector.tensor_copy(
+            wa_codes[:].bitcast(I32).rearrange("p (g t u w) -> p g t u w", g=4, t=4, w=2),
+            wa_raw[:].bitcast(I32).rearrange("p (g u t w) -> p g t u w", g=4, t=4, w=2),
+        )
+        wa_sc = held([P, 2048], U8, "wa_sc")
+        nc.vector.tensor_copy(
+            wa_sc[:].bitcast(I32).rearrange("p (g t u) -> p g t u", g=4, t=4),
+            was_raw[:].bitcast(I32).rearrange("p (g u t) -> p g t u", g=4, t=4),
+        )
+
+        wc_raw = []
+        for b, tag in enumerate(("after_wa", "after_moves")):
+            wc_raw.append(held([P, 4, N], F32, "wc_raw%d" % b, tag=tag)[:])
+            rows = wc[512 * b : 512 * (b + 1), :].rearrange("(u t e) n -> e u t n", t=4, e=4)
+            for e in range(4):
+                nc.sync.dma_start(wc_raw[b][e:P:4, :, :], rows[e])
+
+        def quantise_weight(raw_view, grouped_pattern, quarters, name):
+            grouped = ring.tile([P, 2048], BF16, name=name + "_bf", tag="w_bf", align_bytes=64)
+            for engine_copy, lo, hi in ((nc.scalar.copy, 0, quarters), (nc.vector.tensor_copy, quarters, 4)):
+                if lo < hi:
+                    engine_copy(grouped_pattern(grouped[:, 512 * lo : 512 * hi], hi - lo), raw_view(lo, hi))
+            codes = held([P, 512], U32, name + "_codes")
+            scales = held([P, 512], U8, name + "_scales")
+            nc.vector.quantize_mx(out=codes[:].bitcast(FP8X4), scales=scales[:], in_=grouped[:])
+            return codes, scales
+
+        wb_q = {}
+        for b in range(2):
+            for a in range(2):
+                src = wb_raw[a, b].rearrange("p j (u t e) -> p t u j e", t=4, e=4)
+                wb_q[a, b] = quantise_weight(
+                    lambda lo, hi, src=src: src[:, lo:hi, :, :, :],
+                    lambda dst, n: dst.rearrange("p (t u e j) -> p t u j e", t=n, e=4, j=4),
+                    WB_SCALAR_QUARTERS[2 * b + a],
+                    "wb%d%d" % (a, b),
+                )
+        dispatch = held([P, S + 8], F32, "dispatch", tag="after_word_gather")
+        wgo_sb = dispatch[:, :S]
+        nc.sync.dma_start(wgo_sb, wgo)
+        low_sb = dispatch[:, S : S + 4]
+        nc.sync.dma_start(low_sb, low.rearrange("(p i) -> p i", i=4))
+        wc_q = []
+        for b in range(2):
+            src = wc_raw[b].rearrange("p j (m i) -> p m j i", i=4)
+            wc_q.append(
+                quantise_weight(
+                    lambda lo, hi, src=src: src[:, :, :, lo:hi],
+                    lambda dst, n: dst.rearrange("p (i m j) -> p m j i", i=n, j=4),
+                    WC_SCALAR_QUARTERS[b],
+                    "wc%d" % b,
+                )
+            )
+
+        starts = [sum(GROUPS[:g]) for g in range(len(GROUPS))]
+
+        def first_stage(g):
+            width = GROUPS[g]
+            both = held([P, 16 * width], BF16, "both%d" % g, tag=READINGS_TAG[g])
+            a_bf, b_bf = both[:, : 8 * width], both[:, 8 * width :]
+            for reading, dst in (("a", a_bf), ("b", b_bf)):
+                for j0 in range(0, width, UNIT):
+                    hf, col = divmod(starts[g] + j0, HALF)
+                    for b in range(2):
+                        bank = psum.tile([P, 4, UNIT], F32, name="bank_" + reading, tag="s1" + reading,
+                                         bufs=2 if reading == "a" else 3)
+                        for t in range(4):
+                            for a in range(2):
+                                if reading == "a":
+                                    c = 1024 * a + 512 * b + 128 * t
+                                    lhs = wa_codes[:, 2 * c : 2 * (c + 128)].bitcast(FP4X4)
+                                    lhs_scale = wa_sc[:, c : c + 128]
+                                else:
+                                    lhs = wb_q[a, b][0][:, 128 * t : 128 * (t + 1)].bitcast(FP8X4)
+                                    lhs_scale = wb_q[a, b][1][:, 128 * t : 128 * (t + 1)]
+                                sc0 = starts[g] + j0
+                                nc.tensor.matmul_mx(
+                                    out=bank[:, t, :], lhsT=lhs, lhsT_scale=lhs_scale,
+                                    rhs=v_words[a, hf][:, col : col + UNIT].bitcast(FP8X4),
+                                    rhs_scale=v_scales[a][:, sc0 : sc0 + UNIT],
+                                    start=(a == 0), stop=(a == 1),
+                                )
+                        o = 4 * (width * b + j0)
+                        nc.scalar.copy(
+                            dst[:, o : o + 4 * UNIT].rearrange("p (n t) -> p n t", t=4),
+                            bank[:].rearrange("p t n -> p n t"),
+                        )
+            h_bf = held([P, 8 * width], BF16, "h_bf%d" % g, tag=H_TAG[g])
+            nc.vector.tensor_tensor(h_bf[:], a_bf, b_bf, ALU.min)
+            codes = held([P, 2 * width], U32, "h_codes%d" % g)
+            scales = held([P, 2 * width], U8, "h_scales%d" % g)
+            nc.vector.quantize_mx(out=codes[:].bitcast(FP8X4), scales=scales[:], in_=h_bf[:])
+            return codes, scales
+
+        def second_stage(g, h_q, y_sb, y0):
+            width = GROUPS[g]
+            per_bank = 512 // width
+            for i0 in range(0, 4, per_bank):
+                bank = psum.tile([P, per_bank, width], F32, name="bank_y", tag="s2", bufs=3)
+                for i in range(i0, i0 + per_bank):
+                    for b in range(2):
+                        nc.tensor.matmul_mx(
+                            out=bank[:, i - i0, :],
+                            lhsT=wc_q[b][0][:, 128 * i : 128 * (i + 1)].bitcast(FP8X4),
+                            lhsT_scale=wc_q[b][1][:, 128 * i : 128 * (i + 1)],
+                            rhs=h_q[0][:, width * b : width * (b + 1)].bitcast(FP8X4),
+                            rhs_scale=h_q[1][:, width * b : width * (b + 1)],
+                            start=(b == 0), stop=(b == 1),
+                        )
+                nc.scalar.copy(y_sb[:, i0 : i0 + per_bank, y0 : y0 + width], bank[:])
+
+        pages = [held([P, T2], F32, "page%d" % i) for i in range(4)]
+        out_rows = out.rearrange("(p i) n -> i p n", i=4)
+        READINGS_TAG = ("both0", "both1", "after_moves", "y_sb0", "y_sb1")
+        H_TAG = ("h0", "h1", "h2", "h3", "h4")
+
+        def offers(s, members):
+            j0 = starts[members[0]]
+            width = sum(GROUPS[g] for g in members)
+            y_sb = held([P, 4, width], F32, "y_sb%d" % s)
+            for g in members:
+                second_stage(g, h_q[g], y_sb, starts[g] - j0)
+            return y_sb, j0, width
+
+        def place(y, rows, tag, store):
+            y_sb, j0, width = y
+            raised = held([P, len(rows), width], F32, "raised_" + tag, tag=tag)
+            for n, i in enumerate(rows):
+                nc.vector.tensor_scalar_max(raised[:, n, :], y_sb[:, i, :], low_sb[:, i : i + 1])
+            for n, i in enumerate(rows):
+                nc.vector.tensor_tensor(
+                    pages[i][:].indirect(slots[:, j0 // 16 : (j0 + width) // 16]),
+                    raised[:, n, :], wgo_sb[:, j0 : j0 + width], ALU.mult,
+                )
+                if store:
+                    nc.sync.dma_start(out_rows[i], pages[i][:])
+
+        h_q = {0: first_stage(0)}
+        for i in range(4):
+            (nc.vector if i < 2 else nc.gpsimd).memset(pages[i][:], 0.0)
+        h_q[1] = first_stage(1)
+        y0 = offers(0, (0,))
+        place(y0, (0, 1, 2, 3), "h1", False)
+        y1 = offers(1, (1,))
+        h_q[2] = first_stage(2)
+        place(y1, (0, 1, 2, 3), "h2", False)
+        y2 = offers(2, (2,))
+        h_q[3] = first_stage(3)
+        place(y2, (0, 1), "h3", False)
+        h_q[4] = first_stage(4)
+        place(y2, (2, 3), "h4", False)
+        y3 = offers(3, (3, 4))
+        place(y3, (0, 1), "last_a", True)
+        place(y3, (2, 3), "last_b", True)

@@ -20,8 +20,8 @@ UNIT = 128
 HALF = 512
 GROUPS = (128, 128, 256, 256, 256)
 SCATTERS = ((0,), (1,), (2,), (3, 4))
-WB_SCALAR_QUARTERS = (3, 3, 2, 2)
-WC_SCALAR_QUARTERS = (2, 2)
+WB_SCALAR_QUARTERS = (4, 0, 0, 2)
+WC_SCALAR_QUARTERS = (0, 2)
 
 
 def tile_list_blood_stock_offers_kernel(
@@ -30,7 +30,6 @@ def tile_list_blood_stock_offers_kernel(
     nc = tc.nc
     with ExitStack() as ctx:
         keep = ctx.enter_context(tc.tile_pool(name="keep", bufs=1))
-        ring = ctx.enter_context(tc.tile_pool(name="ring", bufs=2))
         psum = ctx.enter_context(tc.psum_pool(name="psum", bufs=1))
 
         def held(shape, dtype, name, tag=None):
@@ -42,16 +41,16 @@ def tile_list_blood_stock_offers_kernel(
         nc.sync.dma_start(slots[:], offs2)
         scale_table = held([P, T], U8, "scale_table", tag="after_scale_gather")
         nc.gpsimd.memset(scale_table[:].bitcast(I32), 0)
-        word_table = [held([P, T], U32, "word_table0", tag="after_word_gather"), held([P, T], U32, "word_table1")]
+        word_table = [held([P, T], U32, "word_table%d" % a) for a in range(2)]
 
         def load_words(a):
             nc.sync.dma_start(
                 word_table[a][:].bitcast(I32), tab_words[a].rearrange("p n t -> p (n t)").bitcast(I32)
             )
 
-        load_words(0)
         for a in range(2):
             nc.sync.dma_start(scale_table[a:P:8, :].bitcast(I32), tab_scales[a].bitcast(I32))
+        load_words(0)
         load_words(1)
         wa_raw = held([P, 4096], U8, "wa_raw", tag="after_wa")
         nc.sync.dma_start(
@@ -73,30 +72,35 @@ def tile_list_blood_stock_offers_kernel(
                 dst, wb[512 * a : 512 * (a + 1), 512 * b : 512 * (b + 1)].rearrange("(p j) c -> p j c", j=4)
             )
 
-        first_wb = held([P, 4, 512], F32, "first_wb")
-        load_wb(first_wb[:], 0, 0)
-
         picked_scales = held([P, S], U8, "picked_scales", tag="after_moves")
         nc.vector.tensor_copy(picked_scales[:], scale_table[:].indirect(picks[:]))
         nc.vector.tensor_copy(v_scales[0][:].bitcast(I32), picked_scales[:].bitcast(I32))
-        for a, queue, rows in ((0, nc.sync, (1, 2, 3)), (1, nc.sync, (0, 1, 2, 3))):
-            for r in rows:
-                queue.dma_start(
-                    v_scales[a][r:P:32, :].bitcast(I32), picked_scales[8 * r + a : P : 32, :].bitcast(I32)
-                )
-        first_words = held([P, S], U32, "first_words", tag="after_scale_gather")
+        def move_scale_row(a, r):
+            nc.sync.dma_start(v_scales[a][r:P:32, :].bitcast(I32), picked_scales[8 * r + a : P : 32, :].bitcast(I32))
+
+        late = held([P, 4 * 2048], F32, "late", tag="after_scale_gather")
+        wb_raw = {
+            (a, b): late[:, 2048 * (2 * b + a) : 2048 * (2 * b + a + 1)].rearrange("p (j c) -> p j c", j=4)
+            for b in range(2)
+            for a in range(2)
+        }
+        moves = [(1, r) for r in range(4)] + [(0, r) for r in range(1, 4)]
+        move_scale_row(*moves[0])
+        load_wb(wb_raw[0, 0], 0, 0)
+        for a, r in moves[1:]:
+            move_scale_row(a, r)
+        for a, b in ((1, 0), (0, 1), (1, 1)):
+            load_wb(wb_raw[a, b], a, b)
+        first_words = held([P, S], U32, "first_words")
         nc.vector.tensor_copy(first_words[:], word_table[0][:].indirect(picks[:]))
         v_words = {(0, hf): first_words[:, HALF * hf : HALF * (hf + 1)] for hf in range(2)}
-        for hf in range(2):
-            second_words = held([P, HALF], U32, "second_words%d" % hf)
+
+        def gather_second(hf, tag):
+            second_words = held([P, HALF], U32, "second_words%d" % hf, tag=tag)
             nc.vector.tensor_copy(second_words[:], word_table[1][:].indirect(picks[:, 32 * hf : 32 * (hf + 1)]))
             v_words[1, hf] = second_words[:]
 
-        late = held([P, 3 * 2048], F32, "late", tag="after_word_gather")
-        wb_raw = {(0, 0): first_wb[:]}
-        for n, (a, b) in enumerate(((1, 0), (0, 1), (1, 1))):
-            wb_raw[a, b] = late[:, 2048 * n : 2048 * (n + 1)].rearrange("p (j c) -> p j c", j=4)
-            load_wb(wb_raw[a, b], a, b)
+        gather_second(0, None)
 
         wa_codes = held([P, 4096], U8, "wa_codes")
         nc.vector.tensor_copy(
@@ -109,6 +113,7 @@ def tile_list_blood_stock_offers_kernel(
             was_raw[:].bitcast(I32).rearrange("p (g u t) -> p g t u", g=4, t=4),
         )
 
+        gather_second(1, "was_raw")
         wc_raw = []
         for b, tag in enumerate(("after_wa", "after_moves")):
             wc_raw.append(held([P, 4, N], F32, "wc_raw%d" % b, tag=tag)[:])
@@ -117,7 +122,7 @@ def tile_list_blood_stock_offers_kernel(
                 nc.sync.dma_start(wc_raw[b][e:P:4, :, :], rows[e])
 
         def quantise_weight(raw_view, grouped_pattern, quarters, name):
-            grouped = ring.tile([P, 2048], BF16, name=name + "_bf", tag="w_bf", align_bytes=64)
+            grouped = held([P, 2048], BF16, name + "_bf")
             for engine_copy, lo, hi in ((nc.scalar.copy, 0, quarters), (nc.vector.tensor_copy, quarters, 4)):
                 if lo < hi:
                     engine_copy(grouped_pattern(grouped[:, 512 * lo : 512 * hi], hi - lo), raw_view(lo, hi))
@@ -136,7 +141,7 @@ def tile_list_blood_stock_offers_kernel(
                     WB_SCALAR_QUARTERS[2 * b + a],
                     "wb%d%d" % (a, b),
                 )
-        dispatch = held([P, S + 8], F32, "dispatch", tag="after_word_gather")
+        dispatch = held([P, S + 8], F32, "dispatch", tag="after_scale_gather")
         wgo_sb = dispatch[:, :S]
         nc.sync.dma_start(wgo_sb, wgo)
         low_sb = dispatch[:, S : S + 4]
@@ -153,6 +158,7 @@ def tile_list_blood_stock_offers_kernel(
                 )
             )
 
+        first_banks, second_banks = [], []
         starts = [sum(GROUPS[:g]) for g in range(len(GROUPS))]
 
         def first_stage(g):
@@ -163,8 +169,9 @@ def tile_list_blood_stock_offers_kernel(
                 for j0 in range(0, width, UNIT):
                     hf, col = divmod(starts[g] + j0, HALF)
                     for b in range(2):
-                        bank = psum.tile([P, 4, UNIT], F32, name="bank_" + reading, tag="s1" + reading,
-                                         bufs=2 if reading == "a" else 3)
+                        bank = psum.tile([P, 4, UNIT], F32, name="bank_" + reading,
+                                         tag="first%d" % (len(first_banks) % 5))
+                        first_banks.append(bank)
                         for t in range(4):
                             for a in range(2):
                                 if reading == "a":
@@ -197,7 +204,8 @@ def tile_list_blood_stock_offers_kernel(
             width = GROUPS[g]
             per_bank = 512 // width
             for i0 in range(0, 4, per_bank):
-                bank = psum.tile([P, per_bank, width], F32, name="bank_y", tag="s2", bufs=3)
+                bank = psum.tile([P, per_bank, width], F32, name="bank_y", tag="second%d" % (len(second_banks) % 3))
+                second_banks.append(bank)
                 for i in range(i0, i0 + per_bank):
                     for b in range(2):
                         nc.tensor.matmul_mx(
@@ -213,7 +221,7 @@ def tile_list_blood_stock_offers_kernel(
         pages = [held([P, T2], F32, "page%d" % i) for i in range(4)]
         out_rows = out.rearrange("(p i) n -> i p n", i=4)
         READINGS_TAG = ("both0", "both1", "after_moves", "y_sb0", "y_sb1")
-        H_TAG = ("h0", "h1", "h2", "h3", "h4")
+        H_TAG = ("wc0_bf", "wc1_bf", "h2", "h3", "h4")
 
         def offers(s, members):
             j0 = starts[members[0]]
@@ -238,10 +246,10 @@ def tile_list_blood_stock_offers_kernel(
 
         h_q = {0: first_stage(0)}
         for i in range(4):
-            (nc.vector if i < 2 else nc.gpsimd).memset(pages[i][:], 0.0)
+            (nc.vector if i < 1 else nc.gpsimd).memset(pages[i][:], 0.0)
         h_q[1] = first_stage(1)
         y0 = offers(0, (0,))
-        place(y0, (0, 1, 2, 3), "h1", False)
+        place(y0, (0, 1, 2, 3), "wc1_bf", False)
         y1 = offers(1, (1,))
         h_q[2] = first_stage(2)
         place(y1, (0, 1, 2, 3), "h2", False)

@@ -246,7 +246,7 @@ def tile_list_blood_stock_offers_kernel(
 
         h_q = {0: first_stage(0)}
         for i in range(4):
-            (nc.vector if i < 1 else nc.gpsimd).memset(pages[i][:], 0.0)
+            nc.vector.memset(pages[i][:], 0.0)
         h_q[1] = first_stage(1)
         y0 = offers(0, (0,))
         place(y0, (0, 1, 2, 3), "wc1_bf", False)

@@ -20,7 +20,7 @@ UNIT = 128
 HALF = 512
 GROUPS = (128, 128, 256, 256, 256)
 SCATTERS = ((0,), (1,), (2,), (3, 4))
-WB_SCALAR_QUARTERS = (4, 0, 0, 2)
+WB_SCALAR_QUARTERS = (4, 2, 2, 2)
 WC_SCALAR_QUARTERS = (0, 2)
 
 
@@ -218,9 +218,9 @@ def tile_list_blood_stock_offers_kernel(
                         )
                 nc.scalar.copy(y_sb[:, i0 : i0 + per_bank, y0 : y0 + width], bank[:])
 
-        pages = [held([P, T2], F32, "page%d" % i) for i in range(4)]
+        pages = [held([P, T2], F32, "page%d" % i, tag=tag) for i, tag in enumerate((None, None, "word_table1", "wb00_bf"))]
         out_rows = out.rearrange("(p i) n -> i p n", i=4)
-        READINGS_TAG = ("both0", "both1", "after_moves", "y_sb0", "y_sb1")
+        READINGS_TAG = ("wb11_bf", "wb01_bf", "after_moves", "y_sb0", "y_sb1")
         H_TAG = ("wc0_bf", "wc1_bf", "h2", "h3", "h4")
 
         def offers(s, members):

@@ -63,7 +63,7 @@ def tile_list_blood_stock_offers_kernel(
         nc.vector.memset(v_scales[1][:].bitcast(I32), 0)
         was_rows = wa_scales.bitcast(I32).rearrange("a (d r) n -> r d a n", r=4)
         for r in range(4):
-            nc.sync.dma_start(
+            nc.scalar.dma_start(
                 was_raw[r:P:32, :].bitcast(I32).rearrange("p (a n) -> p a n", a=2), was_rows[r]
             )
 
@@ -76,7 +76,7 @@ def tile_list_blood_stock_offers_kernel(
         nc.vector.tensor_copy(picked_scales[:], scale_table[:].indirect(picks[:]))
         nc.vector.tensor_copy(v_scales[0][:].bitcast(I32), picked_scales[:].bitcast(I32))
         def move_scale_row(a, r):
-            nc.sync.dma_start(v_scales[a][r:P:32, :].bitcast(I32), picked_scales[8 * r + a : P : 32, :].bitcast(I32))
+            nc.scalar.dma_start(v_scales[a][r:P:32, :].bitcast(I32), picked_scales[8 * r + a : P : 32, :].bitcast(I32))
 
         late = held([P, 4 * 2048], F32, "late", tag="after_scale_gather")
         wb_raw = {

@@ -17,11 +17,12 @@ ALU = mybir.AluOpType
 
 P = 128
 UNIT = 128
-HALF = 512
-GROUPS = (128, 128, 256, 256, 256)
-SCATTERS = ((0,), (1,), (2,), (3, 4))
-WB_SCALAR_QUARTERS = (4, 2, 2, 2)
-WC_SCALAR_QUARTERS = (0, 2)
+GROUPS = (128, 128, 128, 128, 256, 256)
+RING = 5
+WGO_FIRST = 256
+EARLY = 256
+WB_SCALAR_U = (128, 128, 0, 48)
+WC_SCALAR_M = (0, 44)
 
 
 def tile_list_blood_stock_offers_kernel(
@@ -41,26 +42,20 @@ def tile_list_blood_stock_offers_kernel(
         nc.sync.dma_start(slots[:], offs2)
         scale_table = held([P, T], U8, "scale_table", tag="after_scale_gather")
         nc.gpsimd.memset(scale_table[:].bitcast(I32), 0)
+        for a in range(2):
+            nc.sync.dma_start(scale_table[4 * a : P : 8, :].bitcast(I32), tab_scales[a].bitcast(I32))
         word_table = [held([P, T], U32, "word_table%d" % a) for a in range(2)]
-
-        def load_words(a):
+        for a in range(2):
             nc.sync.dma_start(
                 word_table[a][:].bitcast(I32), tab_words[a].rearrange("p n t -> p (n t)").bitcast(I32)
             )
-
-        for a in range(2):
-            nc.sync.dma_start(scale_table[a:P:8, :].bitcast(I32), tab_scales[a].bitcast(I32))
-        load_words(0)
-        load_words(1)
-        wa_raw = held([P, 4096], U8, "wa_raw", tag="after_wa")
+        wa_raw = held([P, 4096], U8, "wa_raw")
         nc.sync.dma_start(
             wa_raw[:].bitcast(I32).rearrange("p (a n) -> p a n", a=2),
             wa_words.bitcast(I32).rearrange("a p n -> p a n"),
         )
         was_raw = held([P, 2048], U8, "was_raw")
-        nc.vector.memset(was_raw[:].bitcast(I32), 0)
-        v_scales = [held([P, S], U8, "v_scales%d" % a) for a in range(2)]
-        nc.vector.memset(v_scales[1][:].bitcast(I32), 0)
+        nc.gpsimd.memset(was_raw[:].bitcast(I32), 0)
         was_rows = wa_scales.bitcast(I32).rearrange("a (d r) n -> r d a n", r=4)
         for r in range(4):
             nc.scalar.dma_start(
@@ -72,140 +67,154 @@ def tile_list_blood_stock_offers_kernel(
                 dst, wb[512 * a : 512 * (a + 1), 512 * b : 512 * (b + 1)].rearrange("(p j) c -> p j c", j=4)
             )
 
-        picked_scales = held([P, S], U8, "picked_scales", tag="after_moves")
-        nc.vector.tensor_copy(picked_scales[:], scale_table[:].indirect(picks[:]))
-        nc.vector.tensor_copy(v_scales[0][:].bitcast(I32), picked_scales[:].bitcast(I32))
-        def move_scale_row(a, r):
-            nc.scalar.dma_start(v_scales[a][r:P:32, :].bitcast(I32), picked_scales[8 * r + a : P : 32, :].bitcast(I32))
-
-        late = held([P, 4 * 2048], F32, "late", tag="after_scale_gather")
-        wb_raw = {
-            (a, b): late[:, 2048 * (2 * b + a) : 2048 * (2 * b + a + 1)].rearrange("p (j c) -> p j c", j=4)
-            for b in range(2)
-            for a in range(2)
-        }
-        moves = [(1, r) for r in range(4)] + [(0, r) for r in range(1, 4)]
-        move_scale_row(*moves[0])
+        wb_first = held([P, 4, 512], F32, "wb_first")
+        wb_raw = {(0, 0): wb_first[:]}
         load_wb(wb_raw[0, 0], 0, 0)
-        for a, r in moves[1:]:
-            move_scale_row(a, r)
-        for a, b in ((1, 0), (0, 1), (1, 1)):
+
+        v_scales = held([P, 2 * S], U8, "v_scales")
+        nc.vector.memset(v_scales[:].bitcast(I32), 0)
+        pages = {i: held([P, T2], F32, "page%d" % i) for i in range(2)}
+        for i in range(2):
+            nc.vector.memset(pages[i][:], 0.0)
+
+        picked_scales = held([P, S], U8, "picked_scales")
+        nc.vector.tensor_copy(picked_scales[:], scale_table[:].indirect(picks[:]))
+        for d in range(4):
+            nc.scalar.dma_start(
+                v_scales[32 * d : 32 * d + 4, :].bitcast(I32),
+                picked_scales[32 * d : 32 * (d + 1) : 4, :].bitcast(I32),
+            )
+        late = held([P, 3 * 2048], F32, "late", tag="after_scale_gather")
+        for n, (a, b) in enumerate(((1, 0), (0, 1), (1, 1))):
+            wb_raw[a, b] = late[:, 2048 * n : 2048 * (n + 1)].rearrange("p (j c) -> p j c", j=4)
             load_wb(wb_raw[a, b], a, b)
         first_words = held([P, S], U32, "first_words")
         nc.vector.tensor_copy(first_words[:], word_table[0][:].indirect(picks[:]))
-        v_words = {(0, hf): first_words[:, HALF * hf : HALF * (hf + 1)] for hf in range(2)}
-
-        def gather_second(hf, tag):
-            second_words = held([P, HALF], U32, "second_words%d" % hf, tag=tag)
-            nc.vector.tensor_copy(second_words[:], word_table[1][:].indirect(picks[:, 32 * hf : 32 * (hf + 1)]))
-            v_words[1, hf] = second_words[:]
-
-        gather_second(0, None)
+        second_head = held([P, EARLY], U32, "second_head")
+        nc.vector.tensor_copy(second_head[:], word_table[1][:].indirect(picks[:, : EARLY // 16]))
 
         wa_codes = held([P, 4096], U8, "wa_codes")
         nc.vector.tensor_copy(
-            wa_codes[:].bitcast(I32).rearrange("p (g t u w) -> p g t u w", g=4, t=4, w=2),
-            wa_raw[:].bitcast(I32).rearrange("p (g u t w) -> p g t u w", g=4, t=4, w=2),
+            wa_codes[:].bitcast(U16).rearrange("p (g t m) -> p g t m", g=4, t=4),
+            wa_raw[:].bitcast(U16).rearrange("p (g m t) -> p g t m", g=4, t=4),
         )
         wa_sc = held([P, 2048], U8, "wa_sc")
         nc.vector.tensor_copy(
-            wa_sc[:].bitcast(I32).rearrange("p (g t u) -> p g t u", g=4, t=4),
-            was_raw[:].bitcast(I32).rearrange("p (g u t) -> p g t u", g=4, t=4),
+            wa_sc[:].rearrange("p (g t m) -> p g t m", g=4, t=4),
+            was_raw[:].rearrange("p (g m t) -> p g t m", g=4, t=4),
         )
+        second_rest = held([P, S - EARLY], U32, "second_rest", tag="wa_raw")
+        nc.vector.tensor_copy(second_rest[:], word_table[1][:].indirect(picks[:, EARLY // 16 :]))
 
-        gather_second(1, "was_raw")
-        wc_raw = []
-        for b, tag in enumerate(("after_wa", "after_moves")):
-            wc_raw.append(held([P, 4, N], F32, "wc_raw%d" % b, tag=tag)[:])
-            rows = wc[512 * b : 512 * (b + 1), :].rearrange("(u t e) n -> e u t n", t=4, e=4)
-            for e in range(4):
-                nc.sync.dma_start(wc_raw[b][e:P:4, :, :], rows[e])
+        def v_words(a, col):
+            if a == 0:
+                return first_words[:, col : col + UNIT]
+            if col < EARLY:
+                return second_head[:, col : col + UNIT]
+            return second_rest[:, col - EARLY : col - EARLY + UNIT]
 
-        def quantise_weight(raw_view, grouped_pattern, quarters, name):
-            grouped = held([P, 2048], BF16, name + "_bf")
-            for engine_copy, lo, hi in ((nc.scalar.copy, 0, quarters), (nc.vector.tensor_copy, quarters, 4)):
+        def late_page(i, tag):
+            pages[i] = held([P, T2], F32, "page%d" % i, tag=tag)
+            nc.vector.memset(pages[i][:], 0.0)
+
+        late_page(2, "word_table1")
+
+        def round_weight(src, dst, scalar_share, whole):
+            for engine_copy, lo, hi in ((nc.scalar.copy, 0, scalar_share), (nc.vector.tensor_copy, scalar_share, whole)):
                 if lo < hi:
-                    engine_copy(grouped_pattern(grouped[:, 512 * lo : 512 * hi], hi - lo), raw_view(lo, hi))
-            codes = held([P, 512], U32, name + "_codes")
-            scales = held([P, 512], U8, name + "_scales")
-            nc.vector.quantize_mx(out=codes[:].bitcast(FP8X4), scales=scales[:], in_=grouped[:])
+                    engine_copy(dst(lo, hi), src(lo, hi))
+
+        def quantise(grouped, name, tag=None):
+            width = grouped.shape[1] // 4
+            codes = held([P, width], U32, name + "_codes", tag=tag)
+            scales = held([P, width], U8, name + "_scales")
+            nc.vector.quantize_mx(out=codes[:].bitcast(FP8X4), scales=scales[:], in_=grouped)
             return codes, scales
 
         wb_q = {}
-        for b in range(2):
-            for a in range(2):
-                src = wb_raw[a, b].rearrange("p j (u t e) -> p t u j e", t=4, e=4)
-                wb_q[a, b] = quantise_weight(
-                    lambda lo, hi, src=src: src[:, lo:hi, :, :, :],
-                    lambda dst, n: dst.rearrange("p (t u e j) -> p t u j e", t=n, e=4, j=4),
-                    WB_SCALAR_QUARTERS[2 * b + a],
-                    "wb%d%d" % (a, b),
-                )
-        dispatch = held([P, S + 8], F32, "dispatch", tag="after_scale_gather")
-        wgo_sb = dispatch[:, :S]
-        nc.sync.dma_start(wgo_sb, wgo)
-        low_sb = dispatch[:, S : S + 4]
-        nc.sync.dma_start(low_sb, low.rearrange("(p i) -> p i", i=4))
-        wc_q = []
-        for b in range(2):
+
+        def prepare_wb(a, b):
+            grouped = held([P, 2048], BF16, "wb%d%d_bf" % (a, b))
+            src = wb_raw[a, b].rearrange("p j (m t) -> p m j t", t=4)
+            dst = grouped[:].rearrange("p (t m j) -> p m j t", t=4, j=4)
+            round_weight(
+                lambda lo, hi: src[:, lo:hi, :, :], lambda lo, hi: dst[:, lo:hi, :, :], WB_SCALAR_U[2 * b + a], 128
+            )
+            wb_q[a, b] = quantise(grouped[:], "wb%d%d" % (a, b))
+
+        wc_raw = []
+
+        def load_wc(b, tag):
+            wc_raw.append(held([P, 4, N], F32, "wc_raw%d" % b, tag=tag)[:])
+            nc.sync.dma_start(wc_raw[b], wc[512 * b : 512 * (b + 1), :].rearrange("(p j) n -> p j n", j=4))
+
+        def round_wc(b):
+            grouped = held([P, 2048], BF16, "wc%d_bf" % b)
             src = wc_raw[b].rearrange("p j (m i) -> p m j i", i=4)
-            wc_q.append(
-                quantise_weight(
-                    lambda lo, hi, src=src: src[:, :, :, lo:hi],
-                    lambda dst, n: dst.rearrange("p (i m j) -> p m j i", i=n, j=4),
-                    WC_SCALAR_QUARTERS[b],
-                    "wc%d" % b,
-                )
+            dst = grouped[:].rearrange("p (i m j) -> p m j i", i=4, j=4)
+            round_weight(lambda lo, hi: src[:, lo:hi, :, :], lambda lo, hi: dst[:, lo:hi, :, :], WC_SCALAR_M[b], 128)
+            return grouped[:]
+
+        load_wc(0, "word_table0")
+        prepare_wb(0, 0)
+        load_wc(1, "wb_first")
+        late_page(3, "wb00_bf")
+        prepare_wb(1, 0)
+        prepare_wb(0, 1)
+        wgo_sb = late[:, 2048 : 2048 + S]
+        low_sb = late[:, 2048 + S : 2048 + S + 4]
+        nc.sync.dma_start(low_sb, low.rearrange("(p i) -> p i", i=4))
+        nc.sync.dma_start(wgo_sb[:, :WGO_FIRST], wgo[:, :WGO_FIRST])
+        nc.sync.dma_start(wgo_sb[:, WGO_FIRST:], wgo[:, WGO_FIRST:])
+        prepare_wb(1, 1)
+
+        starts = [sum(GROUPS[:g]) for g in range(len(GROUPS))]
+        banks = [psum.tile([P, 512], F32, name="bank%d" % n) for n in range(RING + 2)]
+        ring = []
+
+        def one_bank(g, both, reading, b, j0):
+            width = GROUPS[g]
+            col = starts[g] + j0
+            ring.append(banks[len(ring) % RING])
+            bank = ring[-1][:].rearrange("p (t n) -> p t n", t=4)
+            for t in range(4):
+                for a in range(2):
+                    if reading == 0:
+                        c = 1024 * a + 512 * b + 128 * t
+                        lhs = wa_codes[:, 2 * c : 2 * (c + 128)].bitcast(FP4X4)
+                        lhs_scale = wa_sc[:, c : c + 128]
+                    else:
+                        lhs = wb_q[a, b][0][:, 128 * t : 128 * (t + 1)].bitcast(FP8X4)
+                        lhs_scale = wb_q[a, b][1][:, 128 * t : 128 * (t + 1)]
+                    nc.tensor.matmul_mx(
+                        out=bank[:, t, :], lhsT=lhs, lhsT_scale=lhs_scale,
+                        rhs=v_words(a, col).bitcast(FP8X4),
+                        rhs_scale=v_scales[:, S * a + col : S * a + col + UNIT],
+                        start=(a == 0), stop=(a == 1),
+                    )
+            o = 4 * (width * b + j0)
+            nc.scalar.copy(
+                both[reading][:, o : o + 4 * UNIT].rearrange("p (n t) -> p n t", t=4),
+                bank.rearrange("p t n -> p n t"),
             )
 
-        first_banks, second_banks = [], []
-        starts = [sum(GROUPS[:g]) for g in range(len(GROUPS))]
-
-        def first_stage(g):
-            width = GROUPS[g]
-            both = held([P, 16 * width], BF16, "both%d" % g, tag=READINGS_TAG[g])
-            a_bf, b_bf = both[:, : 8 * width], both[:, 8 * width :]
-            for reading, dst in (("a", a_bf), ("b", b_bf)):
-                for j0 in range(0, width, UNIT):
-                    hf, col = divmod(starts[g] + j0, HALF)
+        def readings(g, room):
+            both = (room[:, : 8 * GROUPS[g]], room[:, 8 * GROUPS[g] :])
+            for j0 in range(0, GROUPS[g], UNIT):
+                for reading in range(2):
                     for b in range(2):
-                        bank = psum.tile([P, 4, UNIT], F32, name="bank_" + reading,
-                                         tag="first%d" % (len(first_banks) % 5))
-                        first_banks.append(bank)
-                        for t in range(4):
-                            for a in range(2):
-                                if reading == "a":
-                                    c = 1024 * a + 512 * b + 128 * t
-                                    lhs = wa_codes[:, 2 * c : 2 * (c + 128)].bitcast(FP4X4)
-                                    lhs_scale = wa_sc[:, c : c + 128]
-                                else:
-                                    lhs = wb_q[a, b][0][:, 128 * t : 128 * (t + 1)].bitcast(FP8X4)
-                                    lhs_scale = wb_q[a, b][1][:, 128 * t : 128 * (t + 1)]
-                                sc0 = starts[g] + j0
-                                nc.tensor.matmul_mx(
-                                    out=bank[:, t, :], lhsT=lhs, lhsT_scale=lhs_scale,
-                                    rhs=v_words[a, hf][:, col : col + UNIT].bitcast(FP8X4),
-                                    rhs_scale=v_scales[a][:, sc0 : sc0 + UNIT],
-                                    start=(a == 0), stop=(a == 1),
-                                )
-                        o = 4 * (width * b + j0)
-                        nc.scalar.copy(
-                            dst[:, o : o + 4 * UNIT].rearrange("p (n t) -> p n t", t=4),
-                            bank[:].rearrange("p t n -> p n t"),
-                        )
-            h_bf = held([P, 8 * width], BF16, "h_bf%d" % g, tag=H_TAG[g])
-            nc.vector.tensor_tensor(h_bf[:], a_bf, b_bf, ALU.min)
-            codes = held([P, 2 * width], U32, "h_codes%d" % g)
-            scales = held([P, 2 * width], U8, "h_scales%d" % g)
-            nc.vector.quantize_mx(out=codes[:].bitcast(FP8X4), scales=scales[:], in_=h_bf[:])
-            return codes, scales
+                        one_bank(g, both, reading, b, j0)
+            return both
 
-        def second_stage(g, h_q, y_sb, y0):
+        def lower(g, both, h_bf):
+            nc.vector.tensor_tensor(h_bf, both[0], both[1], ALU.min)
+            return h_bf
+
+        def second_stage(g, h_q, pieces, free):
             width = GROUPS[g]
             per_bank = 512 // width
-            for i0 in range(0, 4, per_bank):
-                bank = psum.tile([P, per_bank, width], F32, name="bank_y", tag="second%d" % (len(second_banks) % 3))
-                second_banks.append(bank)
+            for n, i0 in enumerate(range(0, 4, per_bank)):
+                bank = free[n][:].rearrange("p (i n) -> p i n", i=per_bank)
                 for i in range(i0, i0 + per_bank):
                     for b in range(2):
                         nc.tensor.matmul_mx(
@@ -216,26 +225,20 @@ def tile_list_blood_stock_offers_kernel(
                             rhs_scale=h_q[1][:, width * b : width * (b + 1)],
                             start=(b == 0), stop=(b == 1),
                         )
-                nc.scalar.copy(y_sb[:, i0 : i0 + per_bank, y0 : y0 + width], bank[:])
+                for lo, hi, dst in pieces:
+                    if i0 <= lo < i0 + per_bank:
+                        nc.scalar.copy(dst, bank[:, lo - i0 : hi - i0, :])
 
-        pages = [held([P, T2], F32, "page%d" % i, tag=tag) for i, tag in enumerate((None, None, "word_table1", "wb00_bf"))]
         out_rows = out.rearrange("(p i) n -> i p n", i=4)
-        READINGS_TAG = ("wb11_bf", "wb01_bf", "after_moves", "y_sb0", "y_sb1")
-        H_TAG = ("wc0_bf", "wc1_bf", "h2", "h3", "h4")
 
-        def offers(s, members):
-            j0 = starts[members[0]]
-            width = sum(GROUPS[g] for g in members)
-            y_sb = held([P, 4, width], F32, "y_sb%d" % s)
-            for g in members:
-                second_stage(g, h_q[g], y_sb, starts[g] - j0)
-            return y_sb, j0, width
+        def raise_rows(y_rows, name):
+            raised = held([P, len(y_rows), list(y_rows.values())[0].shape[1]], F32, name)
+            for n, i in enumerate(y_rows):
+                nc.vector.tensor_scalar_max(raised[:, n, :], y_rows[i], low_sb[:, i : i + 1])
+            return raised
 
-        def place(y, rows, tag, store):
-            y_sb, j0, width = y
-            raised = held([P, len(rows), width], F32, "raised_" + tag, tag=tag)
-            for n, i in enumerate(rows):
-                nc.vector.tensor_scalar_max(raised[:, n, :], y_sb[:, i, :], low_sb[:, i : i + 1])
+        def place(raised, rows, j0, store):
+            width = raised.shape[2]
             for n, i in enumerate(rows):
                 nc.vector.tensor_tensor(
                     pages[i][:].indirect(slots[:, j0 // 16 : (j0 + width) // 16]),
@@ -244,20 +247,56 @@ def tile_list_blood_stock_offers_kernel(
                 if store:
                     nc.sync.dma_start(out_rows[i], pages[i][:])
 
-        h_q = {0: first_stage(0)}
-        for i in range(4):
-            nc.vector.memset(pages[i][:], 0.0)
-        h_q[1] = first_stage(1)
-        y0 = offers(0, (0,))
-        place(y0, (0, 1, 2, 3), "wc1_bf", False)
-        y1 = offers(1, (1,))
-        h_q[2] = first_stage(2)
-        place(y1, (0, 1, 2, 3), "h2", False)
-        y2 = offers(2, (2,))
-        h_q[3] = first_stage(3)
-        place(y2, (0, 1), "h3", False)
-        h_q[4] = first_stage(4)
-        place(y2, (2, 3), "h4", False)
-        y3 = offers(3, (3, 4))
-        place(y3, (0, 1), "last_a", True)
-        place(y3, (2, 3), "last_b", True)
+        def own(g, name, per_column):
+            return held([P, per_column * GROUPS[g]], BF16, "%s%d" % (name, g))[:]
+
+        both = [
+            [late[:, at + 512 * g : at + 512 * (g + 1)].bitcast(BF16) for at in (0, 4096)] for g in range(2)
+        ]
+        for g in range(2):
+            for b in range(2):
+                one_bank(g, both[g], 0, b, 0)
+        for b in range(2):
+            for g in range(2):
+                one_bank(g, both[g], 1, b, 0)
+        wc_bf = round_wc(0)
+        h_bf = lower(0, both[0], wc_raw[0][:, 0, :].bitcast(BF16))
+        wc_q = [quantise(wc_bf, "wc0")]
+        h_q = {0: quantise(h_bf, "h0")}
+        wc_bf = round_wc(1)
+        wc_q.append(quantise(wc_bf, "wc1"))
+        h_q[1] = quantise(lower(1, both[1], wc_bf[:, :1024]), "h1")
+        y_first = held([P, 512], F32, "y_first")
+        y_sb = y_first[:].rearrange("p (i n) -> p i n", i=4)
+        second_stage(0, h_q[0], [(0, 4, y_sb)], ring[-1:])
+        raised = raise_rows({i: y_sb[:, i, :] for i in range(4)}, "raised0")
+
+        place(raised, range(4), 0, False)
+        for g in range(1, 4):
+            h_bf = y_first[:].bitcast(BF16) if g == 1 else own(g + 1, "h_bf", 8)
+            if g == 1:
+                both = wc_raw[1][:, :2, :].rearrange("p j n -> p (j n)").bitcast(BF16)
+            else:
+                both = own(g + 1, "both", 16)
+            lower(g + 1, readings(g + 1, both), h_bf)
+            y_lead = held([P, 1, UNIT], F32, "y_lead%d" % g)
+            y_rest = held([P, 3, UNIT], F32, "y_rest%d" % g)
+            second_stage(g, h_q[g], [(0, 1, y_lead[:]), (1, 4, y_rest[:])], ring[-1:])
+            y_rows = {0: y_lead[:, 0, :], 1: y_rest[:, 0, :], 2: y_rest[:, 1, :], 3: y_rest[:, 2, :]}
+            raised = raise_rows(y_rows, "raised%d" % g)
+            h_q[g + 1] = quantise(h_bf, "h%d" % (g + 1), "y_lead%d" % g)
+            place(raised, range(4), starts[g], False)
+        h_bf = lower(5, readings(5, own(5, "both", 16)), own(5, "h_bf", 8))
+        y_lead = held([P, 1, 256], F32, "y_lead4")
+        y_next = held([P, 1, 256], F32, "y_next4")
+        y_wide = held([P, 2, 512], F32, "y_wide")
+        second_stage(4, h_q[4], [(0, 1, y_lead[:]), (1, 2, y_next[:]), (2, 4, y_wide[:, :, :256])], ring[-2:])
+        raised = raise_rows({0: y_lead[:, 0, :], 1: y_next[:, 0, :]}, "raised4")
+        h_q[5] = quantise(h_bf, "h5", "y_lead4")
+        place(raised, (0, 1), starts[4], False)
+        y_sb = held([P, 2, 256], F32, "y_sb5")
+        second_stage(5, h_q[5], [(0, 2, y_sb[:]), (2, 4, y_wide[:, :, 256:])], banks[RING:])
+        raised = raise_rows({i: y_sb[:, i, :] for i in range(2)}, "raised5")
+        raised_wide = raise_rows({i: y_wide[:, i - 2, :] for i in (2, 3)}, "raised_wide")
+        place(raised, (0, 1), starts[5], True)
+        place(raised_wide, (2, 3), starts[4], True)

@@ -41,7 +41,7 @@ def tile_list_blood_stock_offers_kernel(
         slots = keep.tile([P, S // 16], U16, name="slots")
         nc.sync.dma_start(slots[:], offs2)
         scale_table = held([P, T], U8, "scale_table", tag="after_scale_gather")
-        nc.gpsimd.memset(scale_table[:].bitcast(I32), 0)
+        nc.vector.memset(scale_table[:].bitcast(I32), 0)
         for a in range(2):
             nc.sync.dma_start(scale_table[4 * a : P : 8, :].bitcast(I32), tab_scales[a].bitcast(I32))
         word_table = [held([P, T], U32, "word_table%d" % a) for a in range(2)]
@@ -55,7 +55,7 @@ def tile_list_blood_stock_offers_kernel(
             wa_words.bitcast(I32).rearrange("a p n -> p a n"),
         )
         was_raw = held([P, 2048], U8, "was_raw")
-        nc.gpsimd.memset(was_raw[:].bitcast(I32), 0)
+        nc.vector.memset(was_raw[:].bitcast(I32), 0)
         was_rows = wa_scales.bitcast(I32).rearrange("a (d r) n -> r d a n", r=4)
         for r in range(4):
             nc.scalar.dma_start(

@@ -17,12 +17,9 @@ ALU = mybir.AluOpType
 
 P = 128
 UNIT = 128
-GROUPS = (128, 128, 128, 128, 256, 256)
 RING = 5
-WGO_FIRST = 256
 EARLY = 256
-WB_SCALAR_U = (128, 128, 0, 48)
-WC_SCALAR_M = (0, 44)
+FLOAT_MAX = 3.4028234663852886e38
 
 
 def tile_list_blood_stock_offers_kernel(
@@ -31,29 +28,38 @@ def tile_list_blood_stock_offers_kernel(
     nc = tc.nc
     with ExitStack() as ctx:
         keep = ctx.enter_context(tc.tile_pool(name="keep", bufs=1))
+        laid = ctx.enter_context(tc.tile_pool(name="laid", bufs=1))
         psum = ctx.enter_context(tc.psum_pool(name="psum", bufs=1))
 
         def held(shape, dtype, name, tag=None):
             return keep.tile(shape, dtype, name=name, tag=tag or name, align_bytes=64)
 
+        def placed_at(shape, dtype, name, offset):
+            return laid.tile(shape, dtype, name=name, tag=name, align_bytes=64, offset=offset)
+
         picks = keep.tile([P, S // 16], U16, name="picks")
         nc.sync.dma_start(picks[:], offs)
         slots = keep.tile([P, S // 16], U16, name="slots")
         nc.sync.dma_start(slots[:], offs2)
-        scale_table = held([P, T], U8, "scale_table", tag="after_scale_gather")
+        scale_table = placed_at([P, T], U8, "scale_table", 12288 + 7168)
         nc.vector.memset(scale_table[:].bitcast(I32), 0)
-        for a in range(2):
-            nc.sync.dma_start(scale_table[4 * a : P : 8, :].bitcast(I32), tab_scales[a].bitcast(I32))
+        nc.sync.dma_start(
+            scale_table[0:P:4, :].bitcast(I32), tab_scales.bitcast(I32).rearrange("a q n -> q a n")
+        )
         word_table = [held([P, T], U32, "word_table%d" % a) for a in range(2)]
-        for a in range(2):
+
+        def load_words(a):
             nc.sync.dma_start(
                 word_table[a][:].bitcast(I32), tab_words[a].rearrange("p n t -> p (n t)").bitcast(I32)
             )
-        wa_raw = held([P, 4096], U8, "wa_raw")
+
+        load_words(0)
+        wa_raw = placed_at([P, 4096], U8, "wa_raw", 6144)
         nc.sync.dma_start(
             wa_raw[:].bitcast(I32).rearrange("p (a n) -> p a n", a=2),
             wa_words.bitcast(I32).rearrange("a p n -> p a n"),
         )
+        load_words(1)
         was_raw = held([P, 2048], U8, "was_raw")
         nc.vector.memset(was_raw[:].bitcast(I32), 0)
         was_rows = wa_scales.bitcast(I32).rearrange("a (d r) n -> r d a n", r=4)
@@ -62,18 +68,18 @@ def tile_list_blood_stock_offers_kernel(
                 was_raw[r:P:32, :].bitcast(I32).rearrange("p (a n) -> p a n", a=2), was_rows[r]
             )
 
-        def load_wb(dst, a, b):
-            nc.sync.dma_start(
-                dst, wb[512 * a : 512 * (a + 1), 512 * b : 512 * (b + 1)].rearrange("(p j) c -> p j c", j=4)
-            )
+        def load_rows(dst, src):
+            nc.sync.dma_start(dst.rearrange("p (j c) -> p j c", j=4), src.rearrange("(p j) c -> p j c", j=4))
 
-        wb_first = held([P, 4, 512], F32, "wb_first")
-        wb_raw = {(0, 0): wb_first[:]}
-        load_wb(wb_raw[0, 0], 0, 0)
+        wb_first = held([P, 2048], F32, "wb_first")
+        raw = {"wb00": wb_first[:]}
+        load_rows(raw["wb00"], wb[0:512, 0:512])
+        raw["wb10"] = held([P, 2048], F32, "wb_second")[:]
+        load_rows(raw["wb10"], wb[512:, :512])
 
         v_scales = held([P, 2 * S], U8, "v_scales")
         nc.vector.memset(v_scales[:].bitcast(I32), 0)
-        pages = {i: held([P, T2], F32, "page%d" % i) for i in range(2)}
+        pages = [held([P, T2], F32, "page%d" % i) for i in range(2)]
         for i in range(2):
             nc.vector.memset(pages[i][:], 0.0)
 
@@ -84,27 +90,42 @@ def tile_list_blood_stock_offers_kernel(
                 v_scales[32 * d : 32 * d + 4, :].bitcast(I32),
                 picked_scales[32 * d : 32 * (d + 1) : 4, :].bitcast(I32),
             )
-        late = held([P, 3 * 2048], F32, "late", tag="after_scale_gather")
-        for n, (a, b) in enumerate(((1, 0), (0, 1), (1, 1))):
-            wb_raw[a, b] = late[:, 2048 * n : 2048 * (n + 1)].rearrange("p (j c) -> p j c", j=4)
-            load_wb(wb_raw[a, b], a, b)
+        pages.append(placed_at([P, T2], F32, "page2", 12288))
+        nc.gpsimd.memset(pages[2][:], 0.0)
+
+        late = placed_at([P, 4 * 2048 + S + 16], F32, "late", 12288 + 8192)
+        pieces = (
+            ("wb01", wb[:512, 512:]), ("wb11", wb[512:, 512:]),
+            ("wc0", wc[:512, :]), ("wc1", wc[512:, :]),
+        )
+        for n, (name, src) in enumerate(pieces):
+            raw[name] = late[:, 2048 * n : 2048 * (n + 1)]
+            load_rows(raw[name], src)
+        wgo_sb = late[:, 4 * 2048 : 4 * 2048 + S]
+        low_sb = late[:, 4 * 2048 + S : 4 * 2048 + S + 4]
+        nc.sync.dma_start(low_sb, low.rearrange("(p i) -> p i", i=4))
+        nc.sync.dma_start(wgo_sb[:, :EARLY], wgo[:, :EARLY])
+        nc.sync.dma_start(wgo_sb[:, EARLY:], wgo[:, EARLY:])
+
         first_words = held([P, S], U32, "first_words")
         nc.vector.tensor_copy(first_words[:], word_table[0][:].indirect(picks[:]))
-        second_head = held([P, EARLY], U32, "second_head")
-        nc.vector.tensor_copy(second_head[:], word_table[1][:].indirect(picks[:, : EARLY // 16]))
 
-        wa_codes = held([P, 4096], U8, "wa_codes")
-        nc.vector.tensor_copy(
-            wa_codes[:].bitcast(U16).rearrange("p (g t m) -> p g t m", g=4, t=4),
-            wa_raw[:].bitcast(U16).rearrange("p (g m t) -> p g t m", g=4, t=4),
-        )
         wa_sc = held([P, 2048], U8, "wa_sc")
         nc.vector.tensor_copy(
             wa_sc[:].rearrange("p (g t m) -> p g t m", g=4, t=4),
             was_raw[:].rearrange("p (g m t) -> p g t m", g=4, t=4),
         )
-        second_rest = held([P, S - EARLY], U32, "second_rest", tag="wa_raw")
+        wa_codes = held([P, 4096], U8, "wa_codes", tag="was_raw")
+        nc.vector.tensor_copy(
+            wa_codes[:].bitcast(U16).rearrange("p (g t m) -> p g t m", g=4, t=4),
+            wa_raw[:].bitcast(U16).rearrange("p (g m t) -> p g t m", g=4, t=4),
+        )
+        second_head = placed_at([P, EARLY], U32, "second_head", 8192)
+        nc.vector.tensor_copy(second_head[:], word_table[1][:].indirect(picks[:, : EARLY // 16]))
+        second_rest = placed_at([P, S - EARLY], U32, "second_rest", 8192 + 4 * EARLY)
         nc.vector.tensor_copy(second_rest[:], word_table[1][:].indirect(picks[:, EARLY // 16 :]))
+        pages.append(placed_at([P, T2], F32, "page3", 0))
+        nc.gpsimd.memset(pages[3][:], 0.0)
 
         def v_words(a, col):
             if a == 0:
@@ -113,190 +134,192 @@ def tile_list_blood_stock_offers_kernel(
                 return second_head[:, col : col + UNIT]
             return second_rest[:, col - EARLY : col - EARLY + UNIT]
 
-        def late_page(i, tag):
-            pages[i] = held([P, T2], F32, "page%d" % i, tag=tag)
-            nc.vector.memset(pages[i][:], 0.0)
+        grouped, codes, scales = {}, {}, {}
+        for name in raw:
+            grouped[name] = held([P, 2048], BF16, name + "_bf")[:]
+            codes[name] = held([P, 512], U32, name + "_codes")[:]
+            scales[name] = held([P, 512], U8, name + "_scales")[:]
 
-        late_page(2, "word_table1")
+        def round_weight(copy, name, lo, hi):
+            src = raw[name].rearrange("p (j m t) -> p m j t", j=4, t=4)
+            dst = grouped[name].rearrange("p (t m j) -> p m j t", t=4, j=4)
+            copy(dst[:, :, :, lo:hi], src[:, :, :, lo:hi])
 
-        def round_weight(src, dst, scalar_share, whole):
-            for engine_copy, lo, hi in ((nc.scalar.copy, 0, scalar_share), (nc.vector.tensor_copy, scalar_share, whole)):
-                if lo < hi:
-                    engine_copy(dst(lo, hi), src(lo, hi))
+        def quantise(to_codes, to_scales, values):
+            nc.vector.quantize_mx(out=to_codes.bitcast(FP8X4), scales=to_scales, in_=values)
 
-        def quantise(grouped, name, tag=None):
-            width = grouped.shape[1] // 4
-            codes = held([P, width], U32, name + "_codes", tag=tag)
-            scales = held([P, width], U8, name + "_scales")
-            nc.vector.quantize_mx(out=codes[:].bitcast(FP8X4), scales=scales[:], in_=grouped)
-            return codes, scales
-
-        wb_q = {}
-
-        def prepare_wb(a, b):
-            grouped = held([P, 2048], BF16, "wb%d%d_bf" % (a, b))
-            src = wb_raw[a, b].rearrange("p j (m t) -> p m j t", t=4)
-            dst = grouped[:].rearrange("p (t m j) -> p m j t", t=4, j=4)
-            round_weight(
-                lambda lo, hi: src[:, lo:hi, :, :], lambda lo, hi: dst[:, lo:hi, :, :], WB_SCALAR_U[2 * b + a], 128
-            )
-            wb_q[a, b] = quantise(grouped[:], "wb%d%d" % (a, b))
-
-        wc_raw = []
-
-        def load_wc(b, tag):
-            wc_raw.append(held([P, 4, N], F32, "wc_raw%d" % b, tag=tag)[:])
-            nc.sync.dma_start(wc_raw[b], wc[512 * b : 512 * (b + 1), :].rearrange("(p j) n -> p j n", j=4))
-
-        def round_wc(b):
-            grouped = held([P, 2048], BF16, "wc%d_bf" % b)
-            src = wc_raw[b].rearrange("p j (m i) -> p m j i", i=4)
-            dst = grouped[:].rearrange("p (i m j) -> p m j i", i=4, j=4)
-            round_weight(lambda lo, hi: src[:, lo:hi, :, :], lambda lo, hi: dst[:, lo:hi, :, :], WC_SCALAR_M[b], 128)
-            return grouped[:]
-
-        load_wc(0, "word_table0")
-        prepare_wb(0, 0)
-        load_wc(1, "wb_first")
-        late_page(3, "wb00_bf")
-        prepare_wb(1, 0)
-        prepare_wb(0, 1)
-        wgo_sb = late[:, 2048 : 2048 + S]
-        low_sb = late[:, 2048 + S : 2048 + S + 4]
-        nc.sync.dma_start(low_sb, low.rearrange("(p i) -> p i", i=4))
-        nc.sync.dma_start(wgo_sb[:, :WGO_FIRST], wgo[:, :WGO_FIRST])
-        nc.sync.dma_start(wgo_sb[:, WGO_FIRST:], wgo[:, WGO_FIRST:])
-        prepare_wb(1, 1)
-
-        starts = [sum(GROUPS[:g]) for g in range(len(GROUPS))]
-        banks = [psum.tile([P, 512], F32, name="bank%d" % n) for n in range(RING + 2)]
-        ring = []
-
-        def one_bank(g, both, reading, b, j0):
-            width = GROUPS[g]
-            col = starts[g] + j0
-            ring.append(banks[len(ring) % RING])
-            bank = ring[-1][:].rearrange("p (t n) -> p t n", t=4)
-            for t in range(4):
-                for a in range(2):
-                    if reading == 0:
-                        c = 1024 * a + 512 * b + 128 * t
-                        lhs = wa_codes[:, 2 * c : 2 * (c + 128)].bitcast(FP4X4)
-                        lhs_scale = wa_sc[:, c : c + 128]
-                    else:
-                        lhs = wb_q[a, b][0][:, 128 * t : 128 * (t + 1)].bitcast(FP8X4)
-                        lhs_scale = wb_q[a, b][1][:, 128 * t : 128 * (t + 1)]
-                    nc.tensor.matmul_mx(
-                        out=bank[:, t, :], lhsT=lhs, lhsT_scale=lhs_scale,
-                        rhs=v_words(a, col).bitcast(FP8X4),
-                        rhs_scale=v_scales[:, S * a + col : S * a + col + UNIT],
-                        start=(a == 0), stop=(a == 1),
-                    )
-            o = 4 * (width * b + j0)
-            nc.scalar.copy(
-                both[reading][:, o : o + 4 * UNIT].rearrange("p (n t) -> p n t", t=4),
-                bank.rearrange("p t n -> p n t"),
+        def quantise_weight(name, lo, hi):
+            quantise(
+                codes[name][:, P * lo : P * hi], scales[name][:, P * lo : P * hi],
+                grouped[name][:, 512 * lo : 512 * hi],
             )
 
-        def readings(g, room):
-            both = (room[:, : 8 * GROUPS[g]], room[:, 8 * GROUPS[g] :])
-            for j0 in range(0, GROUPS[g], UNIT):
-                for reading in range(2):
-                    for b in range(2):
-                        one_bank(g, both, reading, b, j0)
-            return both
+        def weight_on_vector(name):
+            for lo in (0, 2):
+                round_weight(nc.vector.tensor_copy, name, lo, lo + 2)
+            for lo in (0, 2):
+                quantise_weight(name, lo, lo + 2)
 
-        def lower(g, both, h_bf):
-            nc.vector.tensor_tensor(h_bf, both[0], both[1], ALU.min)
+        banks = [psum.tile([P, 512], F32, name="bank%d" % n) for n in range(RING)]
+        y_banks = [psum.tile([P, 512], F32, name="y_bank%d" % n) for n in range(3)]
+        used = []
+
+        def reading(which, b, units, room):
+            for n, u in enumerate(units):
+                used.append(banks[len(used) % RING])
+                bank = used[-1][:].rearrange("p (t n) -> p t n", t=4)
+                col = UNIT * u
+                for t in range(4):
+                    for a in range(2):
+                        if which == "a":
+                            c = 1024 * a + 512 * b + 128 * t
+                            lhs = wa_codes[:, 2 * c : 2 * (c + 128)].bitcast(FP4X4)
+                            lhs_scale = wa_sc[:, c : c + 128]
+                        else:
+                            name = "wb%d%d" % (a, b)
+                            lhs = codes[name][:, 128 * t : 128 * (t + 1)].bitcast(FP8X4)
+                            lhs_scale = scales[name][:, 128 * t : 128 * (t + 1)]
+                        nc.tensor.matmul_mx(
+                            out=bank[:, t, :], lhsT=lhs, lhsT_scale=lhs_scale,
+                            rhs=v_words(a, col).bitcast(FP8X4),
+                            rhs_scale=v_scales[:, S * a + col : S * a + col + UNIT],
+                            start=(a == 0), stop=(a == 1),
+                        )
+                nc.scalar.copy(
+                    room[:, 512 * n : 512 * (n + 1)].rearrange("p (n t) -> p n t", t=4),
+                    bank.rearrange("p t n -> p n t"),
+                )
+            return room
+
+        def own(name, columns, dtype=BF16):
+            return held([P, columns], dtype, name)[:]
+
+        h_codes = [own("h_codes%d" % b, S, U32) for b in range(2)]
+        h_scales = [own("h_scales%d" % b, S, U8) for b in range(2)]
+
+        def lower(h_bf, from_a, from_b):
+            nc.vector.tensor_tensor(h_bf, from_a, from_b, ALU.min)
             return h_bf
 
-        def second_stage(g, h_q, pieces, free):
-            width = GROUPS[g]
-            per_bank = 512 // width
-            for n, i0 in enumerate(range(0, 4, per_bank)):
-                bank = free[n][:].rearrange("p (i n) -> p i n", i=per_bank)
-                for i in range(i0, i0 + per_bank):
-                    for b in range(2):
-                        nc.tensor.matmul_mx(
-                            out=bank[:, i - i0, :],
-                            lhsT=wc_q[b][0][:, 128 * i : 128 * (i + 1)].bitcast(FP8X4),
-                            lhsT_scale=wc_q[b][1][:, 128 * i : 128 * (i + 1)],
-                            rhs=h_q[0][:, width * b : width * (b + 1)].bitcast(FP8X4),
-                            rhs_scale=h_q[1][:, width * b : width * (b + 1)],
-                            start=(b == 0), stop=(b == 1),
-                        )
-                for lo, hi, dst in pieces:
-                    if i0 <= lo < i0 + per_bank:
-                        nc.scalar.copy(dst, bank[:, lo - i0 : hi - i0, :])
+        def quantise_h(b, first, h_bf):
+            cols = slice(UNIT * first, UNIT * first + h_bf.shape[1] // 4)
+            quantise(h_codes[b][:, cols], h_scales[b][:, cols], h_bf)
+
+        def offers(bank, i, spans):
+            at = 0
+            for j0, width in spans:
+                for b in range(2):
+                    name = "wc%d" % b
+                    nc.tensor.matmul_mx(
+                        out=bank[:, at : at + width],
+                        lhsT=codes[name][:, 128 * i : 128 * (i + 1)].bitcast(FP8X4),
+                        lhsT_scale=scales[name][:, 128 * i : 128 * (i + 1)],
+                        rhs=h_codes[b][:, j0 : j0 + width].bitcast(FP8X4),
+                        rhs_scale=h_scales[b][:, j0 : j0 + width],
+                        start=(b == 0), stop=(b == 1),
+                    )
+                at += width
+            return bank[:, :at]
+
+        def weigh_from_bank(dst, y, i, j0):
+            nc.vector.scalar_tensor_tensor(
+                dst, y, low_sb[:, i : i + 1], wgo_sb[:, j0 : j0 + y.shape[1]], ALU.max, ALU.mult
+            )
+            return dst
+
+        def weigh_on_gpsimd(y_sb, i, j0, name, raised=None):
+            width = y_sb.shape[1]
+            if raised is None:
+                raised = own(name + "_raised", width, F32)
+            nc.gpsimd.tensor_scalar(raised, y_sb, FLOAT_MAX, low_sb[:, i : i + 1], ALU.min, ALU.max)
+            weighed = own(name + "_weighed", width, F32)
+            nc.gpsimd.tensor_tensor(weighed, raised, wgo_sb[:, j0 : j0 + width], ALU.mult)
+            return weighed
+
+        def to_sbuf(y, name):
+            y_sb = own(name, y.shape[1], F32)
+            nc.scalar.copy(y_sb, y)
+            return y_sb
 
         out_rows = out.rearrange("(p i) n -> i p n", i=4)
 
-        def raise_rows(y_rows, name):
-            raised = held([P, len(y_rows), list(y_rows.values())[0].shape[1]], F32, name)
-            for n, i in enumerate(y_rows):
-                nc.vector.tensor_scalar_max(raised[:, n, :], y_rows[i], low_sb[:, i : i + 1])
-            return raised
+        def put(i, j0, values):
+            nc.vector.tensor_copy(
+                pages[i][:].indirect(slots[:, j0 // 16 : (j0 + values.shape[1]) // 16]), values
+            )
 
-        def place(raised, rows, j0, store):
-            width = raised.shape[2]
-            for n, i in enumerate(rows):
-                nc.vector.tensor_tensor(
-                    pages[i][:].indirect(slots[:, j0 // 16 : (j0 + width) // 16]),
-                    raised[:, n, :], wgo_sb[:, j0 : j0 + width], ALU.mult,
-                )
-                if store:
-                    nc.sync.dma_start(out_rows[i], pages[i][:])
+        round_weight(nc.scalar.copy, "wb00", 0, 4)
+        round_weight(nc.vector.tensor_copy, "wb10", 0, 4)
+        quantise_weight("wb00", 0, 4)
+        quantise_weight("wb10", 0, 4)
+        early = raw["wb00"].bitcast(BF16)
+        a0 = reading("a", 0, range(4), early[:, :2048])
+        a1 = reading("a", 1, range(2), early[:, 2048:3072])
+        weight_on_vector("wb01")
+        b0 = reading("b", 0, range(4), own("b0", 2048))
+        weight_on_vector("wb11")
+        h_bf = lower(grouped["wb11"], a0, b0)
+        round_weight(nc.scalar.copy, "wc0", 2, 4)
+        round_weight(nc.vector.tensor_copy, "wc0", 0, 2)
+        quantise_h(0, 0, h_bf)
+        quantise_weight("wc0", 0, 4)
+        b1 = reading("b", 1, range(2), own("b1", 1024))
+        h_bf = lower(grouped["wc0"][:, :1024], a1, b1)
+        round_weight(nc.scalar.copy, "wc1", 2, 4)
+        round_weight(nc.vector.tensor_copy, "wc1", 0, 2)
+        quantise_h(1, 0, h_bf)
+        quantise_weight("wc1", 0, 2)
+        quantise_weight("wc1", 2, 4)
 
-        def own(g, name, per_column):
-            return held([P, per_column * GROUPS[g]], BF16, "%s%d" % (name, g))[:]
+        spans = ((0, 256),)
+        y0 = offers(y_banks[0][:], 0, spans)
+        offers(y_banks[1][:, :256], 1, spans)
+        offers(y_banks[1][:, 256:], 2, spans)
+        y3 = offers(y_banks[2][:], 3, spans)
+        first = weigh_from_bank(own("first", 256, F32), y0, 0, 0)
+        y12 = to_sbuf(y_banks[1][:], "y12")
+        put(0, 0, first)
+        for i in (1, 2):
+            put(i, 0, weigh_on_gpsimd(y12[:, 256 * (i - 1) : 256 * i], i, 0, "r0s%d" % i))
+        room = raw["wc1"].bitcast(BF16)
+        a1 = reading("a", 1, range(2, 5), room[:, :1536])
+        a0 = reading("a", 0, range(4, 5), room[:, 1536:2048])
+        b1 = reading("b", 1, range(2, 5), room[:, 2048:3584])
+        b0 = reading("b", 0, range(4, 5), room[:, 3584:])
+        h1 = lower(own("h1_mid", 1536), a1, b1)
+        h0 = lower(own("h0_mid", 512), a0, b0)
+        last = weigh_from_bank(raw["wc1"][:, 768:1024], y3, 3, 0)
+        quantise_h(1, 2, h1)
+        quantise_h(0, 4, h0)
 
-        both = [
-            [late[:, at + 512 * g : at + 512 * (g + 1)].bitcast(BF16) for at in (0, 4096)] for g in range(2)
-        ]
-        for g in range(2):
-            for b in range(2):
-                one_bank(g, both[g], 0, b, 0)
-        for b in range(2):
-            for g in range(2):
-                one_bank(g, both[g], 1, b, 0)
-        wc_bf = round_wc(0)
-        h_bf = lower(0, both[0], wc_raw[0][:, 0, :].bitcast(BF16))
-        wc_q = [quantise(wc_bf, "wc0")]
-        h_q = {0: quantise(h_bf, "h0")}
-        wc_bf = round_wc(1)
-        wc_q.append(quantise(wc_bf, "wc1"))
-        h_q[1] = quantise(lower(1, both[1], wc_bf[:, :1024]), "h1")
-        y_first = held([P, 512], F32, "y_first")
-        y_sb = y_first[:].rearrange("p (i n) -> p i n", i=4)
-        second_stage(0, h_q[0], [(0, 4, y_sb)], ring[-1:])
-        raised = raise_rows({i: y_sb[:, i, :] for i in range(4)}, "raised0")
+        spans = ((256, 256), (512, 128))
+        y0 = offers(y_banks[0][:], 0, spans)
+        y1 = offers(y_banks[1][:], 1, spans)
+        y3 = offers(y_banks[2][:], 3, spans)
+        put(3, 0, last)
+        first = weigh_from_bank(own("first1", 384, F32), y0, 0, 256)
+        y1 = to_sbuf(y1, "y1_mid")
+        y3 = to_sbuf(y3, "y3_mid")
+        y2 = offers(y_banks[0][:], 2, spans)
+        put(0, 256, first)
+        put(1, 256, weigh_on_gpsimd(y1, 1, 256, "r1s1"))
+        room = own("end_room", 4 * 768, F32)
+        quarter = [room[:, 768 * n : 768 * (n + 1)] for n in range(4)]
+        a0 = reading("a", 0, range(5, 8), quarter[0].bitcast(BF16))
+        b0 = reading("b", 0, range(5, 8), quarter[1].bitcast(BF16))
+        a1 = reading("a", 1, range(5, 8), quarter[2].bitcast(BF16))
+        b1 = reading("b", 1, range(5, 8), quarter[3].bitcast(BF16))
+        h0 = lower(own("h0_end", 1536), a0, b0)
+        h1_end = own("h1_end", 768, F32)
+        h1 = lower(h1_end.bitcast(BF16), a1, b1)
+        third = weigh_from_bank(quarter[2][:, :384], y2, 2, 256)
+        quantise_h(0, 5, h0)
+        quantise_h(1, 5, h1)
 
-        place(raised, range(4), 0, False)
-        for g in range(1, 4):
-            h_bf = y_first[:].bitcast(BF16) if g == 1 else own(g + 1, "h_bf", 8)
-            if g == 1:
-                both = wc_raw[1][:, :2, :].rearrange("p j n -> p (j n)").bitcast(BF16)
-            else:
-                both = own(g + 1, "both", 16)
-            lower(g + 1, readings(g + 1, both), h_bf)
-            y_lead = held([P, 1, UNIT], F32, "y_lead%d" % g)
-            y_rest = held([P, 3, UNIT], F32, "y_rest%d" % g)
-            second_stage(g, h_q[g], [(0, 1, y_lead[:]), (1, 4, y_rest[:])], ring[-1:])
-            y_rows = {0: y_lead[:, 0, :], 1: y_rest[:, 0, :], 2: y_rest[:, 1, :], 3: y_rest[:, 2, :]}
-            raised = raise_rows(y_rows, "raised%d" % g)
-            h_q[g + 1] = quantise(h_bf, "h%d" % (g + 1), "y_lead%d" % g)
-            place(raised, range(4), starts[g], False)
-        h_bf = lower(5, readings(5, own(5, "both", 16)), own(5, "h_bf", 8))
-        y_lead = held([P, 1, 256], F32, "y_lead4")
-        y_next = held([P, 1, 256], F32, "y_next4")
-        y_wide = held([P, 2, 512], F32, "y_wide")
-        second_stage(4, h_q[4], [(0, 1, y_lead[:]), (1, 2, y_next[:]), (2, 4, y_wide[:, :, :256])], ring[-2:])
-        raised = raise_rows({0: y_lead[:, 0, :], 1: y_next[:, 0, :]}, "raised4")
-        h_q[5] = quantise(h_bf, "h5", "y_lead4")
-        place(raised, (0, 1), starts[4], False)
-        y_sb = held([P, 2, 256], F32, "y_sb5")
-        second_stage(5, h_q[5], [(0, 2, y_sb[:]), (2, 4, y_wide[:, :, 256:])], banks[RING:])
-        raised = raise_rows({i: y_sb[:, i, :] for i in range(2)}, "raised5")
-        raised_wide = raise_rows({i: y_wide[:, i - 2, :] for i in (2, 3)}, "raised_wide")
-        place(raised, (0, 1), starts[5], True)
-        place(raised_wide, (2, 3), starts[4], True)
+        spans = ((640, 128), (768, 256))
+        put(2, 256, third)
+        put(3, 256, weigh_on_gpsimd(y3, 3, 256, "r1s3", h1_end[:, :384]))
+        for i in range(4):
+            y = to_sbuf(offers(y_banks[(i + 1) % 3][:], i, spans), "y%d_end" % i)
+            put(i, 640, weigh_on_gpsimd(y, i, 640, "r2s%d" % i))
+            nc.sync.dma_start(out_rows[i], pages[i][:])

@@ -41,12 +41,12 @@ def tile_list_blood_stock_offers_kernel(
         nc.sync.dma_start(picks[:], offs)
         slots = keep.tile([P, S // 16], U16, name="slots")
         nc.sync.dma_start(slots[:], offs2)
-        scale_table = placed_at([P, T], U8, "scale_table", 12288 + 7168)
+        scale_table = held([P, T], U8, "scale_table")
         nc.vector.memset(scale_table[:].bitcast(I32), 0)
         nc.sync.dma_start(
             scale_table[0:P:4, :].bitcast(I32), tab_scales.bitcast(I32).rearrange("a q n -> q a n")
         )
-        word_table = [held([P, T], U32, "word_table%d" % a) for a in range(2)]
+        word_table = [placed_at([P, T], U32, "word_table0", 16384), held([P, T], U32, "word_table1")]
 
         def load_words(a):
             nc.sync.dma_start(
@@ -54,14 +54,14 @@ def tile_list_blood_stock_offers_kernel(
             )
 
         load_words(0)
-        wa_raw = placed_at([P, 4096], U8, "wa_raw", 6144)
+        wa_raw = held([P, 4096], U8, "wa_raw")
         nc.sync.dma_start(
             wa_raw[:].bitcast(I32).rearrange("p (a n) -> p a n", a=2),
             wa_words.bitcast(I32).rearrange("a p n -> p a n"),
         )
         load_words(1)
-        was_raw = held([P, 2048], U8, "was_raw")
-        nc.vector.memset(was_raw[:].bitcast(I32), 0)
+        was_raw = placed_at([P, 2048], U8, "was_raw", 3072)
+        nc.gpsimd.memset(was_raw[:].bitcast(I32), 0)
         was_rows = wa_scales.bitcast(I32).rearrange("a (d r) n -> r d a n", r=4)
         for r in range(4):
             nc.scalar.dma_start(
@@ -79,9 +79,8 @@ def tile_list_blood_stock_offers_kernel(
 
         v_scales = held([P, 2 * S], U8, "v_scales")
         nc.vector.memset(v_scales[:].bitcast(I32), 0)
-        pages = [held([P, T2], F32, "page%d" % i) for i in range(2)]
-        for i in range(2):
-            nc.vector.memset(pages[i][:], 0.0)
+        pages = [held([P, T2], F32, "page0")]
+        nc.vector.memset(pages[0][:], 0.0)
 
         picked_scales = held([P, S], U8, "picked_scales")
         nc.vector.tensor_copy(picked_scales[:], scale_table[:].indirect(picks[:]))
@@ -90,10 +89,20 @@ def tile_list_blood_stock_offers_kernel(
                 v_scales[32 * d : 32 * d + 4, :].bitcast(I32),
                 picked_scales[32 * d : 32 * (d + 1) : 4, :].bitcast(I32),
             )
-        pages.append(placed_at([P, T2], F32, "page2", 12288))
-        nc.gpsimd.memset(pages[2][:], 0.0)
 
-        late = placed_at([P, 4 * 2048 + S + 16], F32, "late", 12288 + 8192)
+        wa_sc = held([P, 2048], U8, "wa_sc")
+        nc.vector.tensor_copy(
+            wa_sc[:].rearrange("p (g t m) -> p g t m", g=4, t=4),
+            was_raw[:].rearrange("p (g m t) -> p g t m", g=4, t=4),
+        )
+        wa_codes = held([P, 4096], U8, "wa_codes")
+        nc.scalar.copy(
+            wa_codes[:].bitcast(U16).rearrange("p (g t m) -> p g t m", g=4, t=4),
+            wa_raw[:].bitcast(U16).rearrange("p (g m t) -> p g t m", g=4, t=4),
+        )
+        first_words = placed_at([P, S], U32, "first_words", 0)
+        nc.vector.tensor_copy(first_words[:], word_table[0][:].indirect(picks[:]))
+        late = placed_at([P, 4 * 2048 + S + 16], F32, "late", 20480)
         pieces = (
             ("wb01", wb[:512, 512:]), ("wb11", wb[512:, 512:]),
             ("wc0", wc[:512, :]), ("wc1", wc[512:, :]),
@@ -106,26 +115,14 @@ def tile_list_blood_stock_offers_kernel(
         nc.sync.dma_start(low_sb, low.rearrange("(p i) -> p i", i=4))
         nc.sync.dma_start(wgo_sb[:, :EARLY], wgo[:, :EARLY])
         nc.sync.dma_start(wgo_sb[:, EARLY:], wgo[:, EARLY:])
-
-        first_words = held([P, S], U32, "first_words")
-        nc.vector.tensor_copy(first_words[:], word_table[0][:].indirect(picks[:]))
-
-        wa_sc = held([P, 2048], U8, "wa_sc")
-        nc.vector.tensor_copy(
-            wa_sc[:].rearrange("p (g t m) -> p g t m", g=4, t=4),
-            was_raw[:].rearrange("p (g m t) -> p g t m", g=4, t=4),
-        )
-        wa_codes = held([P, 4096], U8, "wa_codes", tag="was_raw")
-        nc.vector.tensor_copy(
-            wa_codes[:].bitcast(U16).rearrange("p (g t m) -> p g t m", g=4, t=4),
-            wa_raw[:].bitcast(U16).rearrange("p (g m t) -> p g t m", g=4, t=4),
-        )
-        second_head = placed_at([P, EARLY], U32, "second_head", 8192)
+        second_head = held([P, EARLY], U32, "second_head")
         nc.vector.tensor_copy(second_head[:], word_table[1][:].indirect(picks[:, : EARLY // 16]))
-        second_rest = placed_at([P, S - EARLY], U32, "second_rest", 8192 + 4 * EARLY)
+        second_rest = held([P, S - EARLY], U32, "second_rest")
         nc.vector.tensor_copy(second_rest[:], word_table[1][:].indirect(picks[:, EARLY // 16 :]))
-        pages.append(placed_at([P, T2], F32, "page3", 0))
-        nc.gpsimd.memset(pages[3][:], 0.0)
+        pages.append(placed_at([P, T2], F32, "page1", 4096))
+        pages.append(placed_at([P, T2], F32, "page2", 12288))
+        for i in (1, 2):
+            nc.gpsimd.memset(pages[i][:], 0.0)
 
         def v_words(a, col):
             if a == 0:
@@ -136,7 +133,8 @@ def tile_list_blood_stock_offers_kernel(
 
         grouped, codes, scales = {}, {}, {}
         for name in raw:
-            grouped[name] = held([P, 2048], BF16, name + "_bf")[:]
+            if name.startswith("wb"):
+                grouped[name] = held([P, 2048], BF16, name + "_bf")[:]
             codes[name] = held([P, 512], U32, name + "_codes")[:]
             scales[name] = held([P, 512], U8, name + "_scales")[:]
 
@@ -248,47 +246,52 @@ def tile_list_blood_stock_offers_kernel(
                 pages[i][:].indirect(slots[:, j0 // 16 : (j0 + values.shape[1]) // 16]), values
             )
 
-        round_weight(nc.scalar.copy, "wb00", 0, 4)
-        round_weight(nc.vector.tensor_copy, "wb10", 0, 4)
-        quantise_weight("wb00", 0, 4)
-        quantise_weight("wb10", 0, 4)
-        early = raw["wb00"].bitcast(BF16)
-        a0 = reading("a", 0, range(4), early[:, :2048])
-        a1 = reading("a", 1, range(2), early[:, 2048:3072])
+        weight_on_vector("wb00")
+        weight_on_vector("wb10")
+        a0_lo = reading("a", 0, range(2), own("a0_lo", 1024))
+        a0_hi = reading("a", 0, range(2, 4), own("a0_hi", 1024))
+        a1 = reading("a", 1, range(2), own("a1", 1024))
+        a0 = reading("a", 0, range(4, 8), own("a0", 2048))
         weight_on_vector("wb01")
         b0 = reading("b", 0, range(4), own("b0", 2048))
         weight_on_vector("wb11")
-        h_bf = lower(grouped["wb11"], a0, b0)
-        round_weight(nc.scalar.copy, "wc0", 2, 4)
+        h_bf = raw["wb11"][:, :1024].bitcast(BF16)
+        lower(h_bf[:, :1024], a0_lo, b0[:, :1024])
+        lower(h_bf[:, 1024:], a0_hi, b0[:, 1024:])
+        grouped["wc0"] = held([P, 2048], BF16, "wc0_bf", tag="a0_lo")[:]
         round_weight(nc.vector.tensor_copy, "wc0", 0, 2)
         quantise_h(0, 0, h_bf)
-        quantise_weight("wc0", 0, 4)
+        quantise_weight("wc0", 0, 2)
         b1 = reading("b", 1, range(2), own("b1", 1024))
-        h_bf = lower(grouped["wc0"][:, :1024], a1, b1)
-        round_weight(nc.scalar.copy, "wc1", 2, 4)
-        round_weight(nc.vector.tensor_copy, "wc1", 0, 2)
+        round_weight(nc.scalar.copy, "wc0", 2, 4)
+        h_bf = lower(raw["wb11"][:, 1024:1536].bitcast(BF16), a1, b1)
         quantise_h(1, 0, h_bf)
+        grouped["wc1"] = held([P, 2048], BF16, "wc1_bf", tag="a1")[:]
+        round_weight(nc.vector.tensor_copy, "wc1", 0, 2)
+        round_weight(nc.scalar.copy, "wc1", 2, 4)
+        quantise_weight("wc0", 2, 4)
         quantise_weight("wc1", 0, 2)
-        quantise_weight("wc1", 2, 4)
 
         spans = ((0, 256),)
         y0 = offers(y_banks[0][:], 0, spans)
-        offers(y_banks[1][:, :256], 1, spans)
-        offers(y_banks[1][:, 256:], 2, spans)
-        y3 = offers(y_banks[2][:], 3, spans)
+        y1 = offers(y_banks[1][:], 1, spans)
         first = weigh_from_bank(own("first", 256, F32), y0, 0, 0)
-        y12 = to_sbuf(y_banks[1][:], "y12")
+        y1 = to_sbuf(y1, "y1_first")
+        quantise_weight("wc1", 2, 4)
+        y2 = to_sbuf(offers(y_banks[0][:], 2, spans), "y2_first")
+        y3 = offers(y_banks[2][:], 3, spans)
         put(0, 0, first)
-        for i in (1, 2):
-            put(i, 0, weigh_on_gpsimd(y12[:, 256 * (i - 1) : 256 * i], i, 0, "r0s%d" % i))
+        put(1, 0, weigh_on_gpsimd(y1, 1, 0, "r0s1"))
+        put(2, 0, weigh_on_gpsimd(y2, 2, 0, "r0s2"))
+        pages.append(held([P, T2], F32, "page3", tag="y2_first"))
+        nc.gpsimd.memset(pages[3][:], 0.0)
         room = raw["wc1"].bitcast(BF16)
         a1 = reading("a", 1, range(2, 5), room[:, :1536])
-        a0 = reading("a", 0, range(4, 5), room[:, 1536:2048])
-        b1 = reading("b", 1, range(2, 5), room[:, 2048:3584])
-        b0 = reading("b", 0, range(4, 5), room[:, 3584:])
+        b1 = reading("b", 1, range(2, 5), room[:, 1536:3072])
+        b0 = reading("b", 0, range(4, 5), room[:, 3072:3584])
         h1 = lower(own("h1_mid", 1536), a1, b1)
-        h0 = lower(own("h0_mid", 512), a0, b0)
-        last = weigh_from_bank(raw["wc1"][:, 768:1024], y3, 3, 0)
+        h0 = lower(own("h0_mid", 512), a0[:, :512], b0)
+        last = weigh_from_bank(raw["wc1"][:, 1536:1792], y3, 3, 0)
         quantise_h(1, 2, h1)
         quantise_h(0, 4, h0)
 
@@ -303,13 +306,12 @@ def tile_list_blood_stock_offers_kernel(
         y2 = offers(y_banks[0][:], 2, spans)
         put(0, 256, first)
         put(1, 256, weigh_on_gpsimd(y1, 1, 256, "r1s1"))
-        room = own("end_room", 4 * 768, F32)
-        quarter = [room[:, 768 * n : 768 * (n + 1)] for n in range(4)]
-        a0 = reading("a", 0, range(5, 8), quarter[0].bitcast(BF16))
+        room = own("end_room", 3 * 768, F32)
+        quarter = [None] + [room[:, 768 * n : 768 * (n + 1)] for n in range(3)]
         b0 = reading("b", 0, range(5, 8), quarter[1].bitcast(BF16))
         a1 = reading("a", 1, range(5, 8), quarter[2].bitcast(BF16))
         b1 = reading("b", 1, range(5, 8), quarter[3].bitcast(BF16))
-        h0 = lower(own("h0_end", 1536), a0, b0)
+        h0 = lower(own("h0_end", 1536), a0[:, 512:], b0)
         h1_end = own("h1_end", 768, F32)
         h1 = lower(h1_end.bitcast(BF16), a1, b1)
         third = weigh_from_bank(quarter[2][:, :384], y2, 2, 256)

@@ -79,8 +79,9 @@ def tile_list_blood_stock_offers_kernel(
 
         v_scales = held([P, 2 * S], U8, "v_scales")
         nc.vector.memset(v_scales[:].bitcast(I32), 0)
-        pages = [held([P, T2], F32, "page0")]
-        nc.vector.memset(pages[0][:], 0.0)
+        pages = [held([P, T2], F32, "page%d" % i) for i in range(2)]
+        for i in range(2):
+            nc.vector.memset(pages[i][:], 0.0)
 
         picked_scales = held([P, S], U8, "picked_scales")
         nc.vector.tensor_copy(picked_scales[:], scale_table[:].indirect(picks[:]))
@@ -119,10 +120,8 @@ def tile_list_blood_stock_offers_kernel(
         nc.vector.tensor_copy(second_head[:], word_table[1][:].indirect(picks[:, : EARLY // 16]))
         second_rest = held([P, S - EARLY], U32, "second_rest")
         nc.vector.tensor_copy(second_rest[:], word_table[1][:].indirect(picks[:, EARLY // 16 :]))
-        pages.append(placed_at([P, T2], F32, "page1", 4096))
-        pages.append(placed_at([P, T2], F32, "page2", 12288))
-        for i in (1, 2):
-            nc.gpsimd.memset(pages[i][:], 0.0)
+        pages.append(placed_at([P, T2], F32, "page2", 4096))
+        nc.gpsimd.memset(pages[2][:], 0.0)
 
         def v_words(a, col):
             if a == 0:

@@ -39,6 +39,11 @@ def tile_list_blood_stock_offers_kernel(
 
         picks = keep.tile([P, S // 16], U16, name="picks")
         nc.sync.dma_start(picks[:], offs)
+        wa_raw = held([P, 4096], U8, "wa_raw")
+        nc.sync.dma_start(
+            wa_raw[:].bitcast(I32).rearrange("p (a n) -> p a n", a=2),
+            wa_words.bitcast(I32).rearrange("a p n -> p a n"),
+        )
         slots = keep.tile([P, S // 16], U16, name="slots")
         nc.sync.dma_start(slots[:], offs2)
         scale_table = held([P, T], U8, "scale_table")
@@ -54,13 +59,8 @@ def tile_list_blood_stock_offers_kernel(
             )
 
         load_words(0)
-        wa_raw = held([P, 4096], U8, "wa_raw")
-        nc.sync.dma_start(
-            wa_raw[:].bitcast(I32).rearrange("p (a n) -> p a n", a=2),
-            wa_words.bitcast(I32).rearrange("a p n -> p a n"),
-        )
         load_words(1)
-        was_raw = placed_at([P, 2048], U8, "was_raw", 3072)
+        was_raw = placed_at([P, 2048], U8, "was_raw", 7168)
         nc.gpsimd.memset(was_raw[:].bitcast(I32), 0)
         was_rows = wa_scales.bitcast(I32).rearrange("a (d r) n -> r d a n", r=4)
         for r in range(4):
@@ -74,8 +74,6 @@ def tile_list_blood_stock_offers_kernel(
         wb_first = held([P, 2048], F32, "wb_first")
         raw = {"wb00": wb_first[:]}
         load_rows(raw["wb00"], wb[0:512, 0:512])
-        raw["wb10"] = held([P, 2048], F32, "wb_second")[:]
-        load_rows(raw["wb10"], wb[512:, :512])
 
         v_scales = held([P, 2 * S], U8, "v_scales")
         nc.vector.memset(v_scales[:].bitcast(I32), 0)
@@ -91,7 +89,7 @@ def tile_list_blood_stock_offers_kernel(
                 picked_scales[32 * d : 32 * (d + 1) : 4, :].bitcast(I32),
             )
 
-        wa_sc = held([P, 2048], U8, "wa_sc")
+        wa_sc = held([P, 2048], U8, "wa_sc", tag="scale_table")
         nc.vector.tensor_copy(
             wa_sc[:].rearrange("p (g t m) -> p g t m", g=4, t=4),
             was_raw[:].rearrange("p (g m t) -> p g t m", g=4, t=4),
@@ -101,7 +99,9 @@ def tile_list_blood_stock_offers_kernel(
             wa_codes[:].bitcast(U16).rearrange("p (g t m) -> p g t m", g=4, t=4),
             wa_raw[:].bitcast(U16).rearrange("p (g m t) -> p g t m", g=4, t=4),
         )
-        first_words = placed_at([P, S], U32, "first_words", 0)
+        raw["wb10"] = placed_at([P, 2048], F32, "wb_second", 0)[:]
+        load_rows(raw["wb10"], wb[512:, :512])
+        first_words = held([P, S], U32, "first_words")
         nc.vector.tensor_copy(first_words[:], word_table[0][:].indirect(picks[:]))
         late = placed_at([P, 4 * 2048 + S + 16], F32, "late", 20480)
         pieces = (
@@ -120,7 +120,7 @@ def tile_list_blood_stock_offers_kernel(
         nc.vector.tensor_copy(second_head[:], word_table[1][:].indirect(picks[:, : EARLY // 16]))
         second_rest = held([P, S - EARLY], U32, "second_rest")
         nc.vector.tensor_copy(second_rest[:], word_table[1][:].indirect(picks[:, EARLY // 16 :]))
-        pages.append(placed_at([P, T2], F32, "page2", 4096))
+        pages.append(placed_at([P, T2], F32, "page2", 8192))
         nc.gpsimd.memset(pages[2][:], 0.0)
 
         def v_words(a, col):
@@ -152,16 +152,14 @@ def tile_list_blood_stock_offers_kernel(
             )
 
         def weight_on_vector(name):
-            for lo in (0, 2):
-                round_weight(nc.vector.tensor_copy, name, lo, lo + 2)
-            for lo in (0, 2):
-                quantise_weight(name, lo, lo + 2)
+            round_weight(nc.vector.tensor_copy, name, 0, 4)
+            quantise_weight(name, 0, 4)
 
         banks = [psum.tile([P, 512], F32, name="bank%d" % n) for n in range(RING)]
         y_banks = [psum.tile([P, 512], F32, name="y_bank%d" % n) for n in range(3)]
         used = []
 
-        def reading(which, b, units, room):
+        def reading(which, b, units, room, against=None):
             for n, u in enumerate(units):
                 used.append(banks[len(used) % RING])
                 bank = used[-1][:].rearrange("p (t n) -> p t n", t=4)
@@ -182,10 +180,15 @@ def tile_list_blood_stock_offers_kernel(
                             rhs_scale=v_scales[:, S * a + col : S * a + col + UNIT],
                             start=(a == 0), stop=(a == 1),
                         )
-                nc.scalar.copy(
-                    room[:, 512 * n : 512 * (n + 1)].rearrange("p (n t) -> p n t", t=4),
-                    bank.rearrange("p t n -> p n t"),
-                )
+                cols = slice(512 * n, 512 * (n + 1))
+                dst = room[:, cols].rearrange("p (n t) -> p n t", t=4)
+                if against is None:
+                    nc.scalar.copy(dst, bank.rearrange("p t n -> p n t"))
+                else:
+                    nc.vector.tensor_tensor(
+                        dst, bank.rearrange("p t n -> p n t"),
+                        against[:, cols].rearrange("p (n t) -> p n t", t=4), ALU.min,
+                    )
             return room
 
         def own(name, columns, dtype=BF16):
@@ -258,13 +261,12 @@ def tile_list_blood_stock_offers_kernel(
         lower(h_bf[:, :1024], a0_lo, b0[:, :1024])
         lower(h_bf[:, 1024:], a0_hi, b0[:, 1024:])
         grouped["wc0"] = held([P, 2048], BF16, "wc0_bf", tag="a0_lo")[:]
-        round_weight(nc.vector.tensor_copy, "wc0", 0, 2)
+        round_weight(nc.scalar.copy, "wc0", 0, 2)
+        h1_bf = reading("b", 1, range(2), raw["wb11"][:, 1024:1536].bitcast(BF16), a1)
         quantise_h(0, 0, h_bf)
+        quantise_h(1, 0, h1_bf)
         quantise_weight("wc0", 0, 2)
-        b1 = reading("b", 1, range(2), own("b1", 1024))
         round_weight(nc.scalar.copy, "wc0", 2, 4)
-        h_bf = lower(raw["wb11"][:, 1024:1536].bitcast(BF16), a1, b1)
-        quantise_h(1, 0, h_bf)
         grouped["wc1"] = held([P, 2048], BF16, "wc1_bf", tag="a1")[:]
         round_weight(nc.vector.tensor_copy, "wc1", 0, 2)
         round_weight(nc.scalar.copy, "wc1", 2, 4)

@@ -248,27 +248,29 @@ def tile_list_blood_stock_offers_kernel(
                 pages[i][:].indirect(slots[:, j0 // 16 : (j0 + values.shape[1]) // 16]), values
             )
 
-        weight_on_vector("wb00")
-        weight_on_vector("wb10")
-        a0_lo = reading("a", 0, range(2), own("a0_lo", 1024))
+        round_weight(nc.scalar.copy, "wb00", 0, 4)
+        round_weight(nc.vector.tensor_copy, "wb10", 0, 4)
+        quantise_weight("wb00", 0, 4)
+        quantise_weight("wb10", 0, 4)
+        a0_lo = reading("a", 0, range(2), raw["wb00"][:, :512].bitcast(BF16))
         a0_hi = reading("a", 0, range(2, 4), own("a0_hi", 1024))
         a1 = reading("a", 1, range(2), own("a1", 1024))
-        a0 = reading("a", 0, range(4, 8), own("a0", 2048))
         weight_on_vector("wb01")
         b0 = reading("b", 0, range(4), own("b0", 2048))
-        weight_on_vector("wb11")
+        round_weight(nc.vector.tensor_copy, "wb11", 0, 4)
         h_bf = raw["wb11"][:, :1024].bitcast(BF16)
         lower(h_bf[:, :1024], a0_lo, b0[:, :1024])
+        quantise_weight("wb11", 0, 4)
         lower(h_bf[:, 1024:], a0_hi, b0[:, 1024:])
-        grouped["wc0"] = held([P, 2048], BF16, "wc0_bf", tag="a0_lo")[:]
+        grouped["wc0"] = raw["wb00"][:, :1024].bitcast(BF16)
         round_weight(nc.scalar.copy, "wc0", 0, 2)
         h1_bf = reading("b", 1, range(2), raw["wb11"][:, 1024:1536].bitcast(BF16), a1)
         quantise_h(0, 0, h_bf)
         quantise_h(1, 0, h1_bf)
         quantise_weight("wc0", 0, 2)
         round_weight(nc.scalar.copy, "wc0", 2, 4)
-        grouped["wc1"] = held([P, 2048], BF16, "wc1_bf", tag="a1")[:]
-        round_weight(nc.vector.tensor_copy, "wc1", 0, 2)
+        grouped["wc1"] = held([P, 2048], BF16, "wc1_bf", tag="a0_hi")[:]
+        round_weight(nc.scalar.copy, "wc1", 0, 2)
         round_weight(nc.scalar.copy, "wc1", 2, 4)
         quantise_weight("wc0", 2, 4)
         quantise_weight("wc1", 0, 2)
@@ -288,10 +290,11 @@ def tile_list_blood_stock_offers_kernel(
         nc.gpsimd.memset(pages[3][:], 0.0)
         room = raw["wc1"].bitcast(BF16)
         a1 = reading("a", 1, range(2, 5), room[:, :1536])
+        a0 = reading("a", 0, range(4, 5), room[:, 3584:])
         b1 = reading("b", 1, range(2, 5), room[:, 1536:3072])
         b0 = reading("b", 0, range(4, 5), room[:, 3072:3584])
         h1 = lower(own("h1_mid", 1536), a1, b1)
-        h0 = lower(own("h0_mid", 512), a0[:, :512], b0)
+        h0 = lower(own("h0_mid", 512), a0, b0)
         last = weigh_from_bank(raw["wc1"][:, 1536:1792], y3, 3, 0)
         quantise_h(1, 2, h1)
         quantise_h(0, 4, h0)
@@ -307,12 +310,13 @@ def tile_list_blood_stock_offers_kernel(
         y2 = offers(y_banks[0][:], 2, spans)
         put(0, 256, first)
         put(1, 256, weigh_on_gpsimd(y1, 1, 256, "r1s1"))
-        room = own("end_room", 3 * 768, F32)
-        quarter = [None] + [room[:, 768 * n : 768 * (n + 1)] for n in range(3)]
+        room = own("end_room", 4 * 768, F32)
+        quarter = [room[:, 768 * n : 768 * (n + 1)] for n in range(4)]
+        a0 = reading("a", 0, range(5, 8), quarter[0].bitcast(BF16))
         b0 = reading("b", 0, range(5, 8), quarter[1].bitcast(BF16))
         a1 = reading("a", 1, range(5, 8), quarter[2].bitcast(BF16))
         b1 = reading("b", 1, range(5, 8), quarter[3].bitcast(BF16))
-        h0 = lower(own("h0_end", 1536), a0[:, 512:], b0)
+        h0 = lower(own("h0_end", 1536), a0, b0)
         h1_end = own("h1_end", 768, F32)
         h1 = lower(h1_end.bitcast(BF16), a1, b1)
         third = weigh_from_bank(quarter[2][:, :384], y2, 2, 256)

@@ -137,10 +137,10 @@ def tile_list_blood_stock_offers_kernel(
             codes[name] = held([P, 512], U32, name + "_codes")[:]
             scales[name] = held([P, 512], U8, name + "_scales")[:]
 
-        def round_weight(copy, name, lo, hi):
+        def round_weight(copy, name, lo, hi, rows=slice(0, P)):
             src = raw[name].rearrange("p (j m t) -> p m j t", j=4, t=4)
             dst = grouped[name].rearrange("p (t m j) -> p m j t", t=4, j=4)
-            copy(dst[:, :, :, lo:hi], src[:, :, :, lo:hi])
+            copy(dst[:, rows, :, lo:hi], src[:, rows, :, lo:hi])
 
         def quantise(to_codes, to_scales, values):
             nc.vector.quantize_mx(out=to_codes.bitcast(FP8X4), scales=to_scales, in_=values)
@@ -248,21 +248,22 @@ def tile_list_blood_stock_offers_kernel(
                 pages[i][:].indirect(slots[:, j0 // 16 : (j0 + values.shape[1]) // 16]), values
             )
 
-        round_weight(nc.scalar.copy, "wb00", 0, 4)
-        round_weight(nc.vector.tensor_copy, "wb10", 0, 4)
+        round_weight(nc.scalar.copy, "wb00", 0, 4, slice(0, 64))
+        round_weight(nc.vector.tensor_copy, "wb00", 0, 4, slice(64, P))
         quantise_weight("wb00", 0, 4)
-        quantise_weight("wb10", 0, 4)
-        a0_lo = reading("a", 0, range(2), raw["wb00"][:, :512].bitcast(BF16))
+        weight_on_vector("wb10")
+        a0_lo = reading("a", 0, range(2), own("a0_lo", 1024))
         a0_hi = reading("a", 0, range(2, 4), own("a0_hi", 1024))
         a1 = reading("a", 1, range(2), own("a1", 1024))
         weight_on_vector("wb01")
         b0 = reading("b", 0, range(4), own("b0", 2048))
-        round_weight(nc.vector.tensor_copy, "wb11", 0, 4)
-        h_bf = raw["wb11"][:, :1024].bitcast(BF16)
+        round_weight(nc.vector.tensor_copy, "wb11", 0, 4, slice(0, 88))
+        round_weight(nc.scalar.copy, "wb11", 0, 4, slice(88, P))
+        h_bf = raw["wb01"][:, :1024].bitcast(BF16)
         lower(h_bf[:, :1024], a0_lo, b0[:, :1024])
         quantise_weight("wb11", 0, 4)
         lower(h_bf[:, 1024:], a0_hi, b0[:, 1024:])
-        grouped["wc0"] = raw["wb00"][:, :1024].bitcast(BF16)
+        grouped["wc0"] = held([P, 2048], BF16, "wc0_bf", tag="a0_lo")[:]
         round_weight(nc.scalar.copy, "wc0", 0, 2)
         h1_bf = reading("b", 1, range(2), raw["wb11"][:, 1024:1536].bitcast(BF16), a1)
         quantise_h(0, 0, h_bf)
@@ -272,8 +273,8 @@ def tile_list_blood_stock_offers_kernel(
         grouped["wc1"] = held([P, 2048], BF16, "wc1_bf", tag="a0_hi")[:]
         round_weight(nc.scalar.copy, "wc1", 0, 2)
         round_weight(nc.scalar.copy, "wc1", 2, 4)
-        quantise_weight("wc0", 2, 4)
         quantise_weight("wc1", 0, 2)
+        quantise_weight("wc0", 2, 4)
 
         spans = ((0, 256),)
         y0 = offers(y_banks[0][:], 0, spans)
@@ -295,8 +296,8 @@ def tile_list_blood_stock_offers_kernel(
         b0 = reading("b", 0, range(4, 5), room[:, 3072:3584])
         h1 = lower(own("h1_mid", 1536), a1, b1)
         h0 = lower(own("h0_mid", 512), a0, b0)
-        last = weigh_from_bank(raw["wc1"][:, 1536:1792], y3, 3, 0)
         quantise_h(1, 2, h1)
+        last = weigh_from_bank(raw["wc1"][:, 1536:1792], y3, 3, 0)
         quantise_h(0, 4, h0)
 
         spans = ((256, 256), (512, 128))
@@ -313,14 +314,16 @@ def tile_list_blood_stock_offers_kernel(
         room = own("end_room", 4 * 768, F32)
         quarter = [room[:, 768 * n : 768 * (n + 1)] for n in range(4)]
         a0 = reading("a", 0, range(5, 8), quarter[0].bitcast(BF16))
-        b0 = reading("b", 0, range(5, 8), quarter[1].bitcast(BF16))
         a1 = reading("a", 1, range(5, 8), quarter[2].bitcast(BF16))
-        b1 = reading("b", 1, range(5, 8), quarter[3].bitcast(BF16))
+        b0, b1 = quarter[1].bitcast(BF16), quarter[3].bitcast(BF16)
+        for n, u in enumerate(range(5, 8)):
+            for b, room_b in enumerate((b0, b1)):
+                reading("b", b, (u,), room_b[:, 512 * n : 512 * (n + 1)])
         h0 = lower(own("h0_end", 1536), a0, b0)
         h1_end = own("h1_end", 768, F32)
         h1 = lower(h1_end.bitcast(BF16), a1, b1)
-        third = weigh_from_bank(quarter[2][:, :384], y2, 2, 256)
         quantise_h(0, 5, h0)
+        third = weigh_from_bank(quarter[2][:, :384], y2, 2, 256)
         quantise_h(1, 5, h1)
 
         spans = ((640, 128), (768, 256))

@@ -19,6 +19,7 @@ P = 128
 UNIT = 128
 RING = 5
 EARLY = 256
+LEAD = 320
 FLOAT_MAX = 3.4028234663852886e38
 
 
@@ -51,7 +52,7 @@ def tile_list_blood_stock_offers_kernel(
         nc.sync.dma_start(
             scale_table[0:P:4, :].bitcast(I32), tab_scales.bitcast(I32).rearrange("a q n -> q a n")
         )
-        word_table = [placed_at([P, T], U32, "word_table0", 16384), held([P, T], U32, "word_table1")]
+        word_table = [held([P, T], U32, "word_table%d" % a) for a in range(2)]
 
         def load_words(a):
             nc.sync.dma_start(
@@ -99,20 +100,18 @@ def tile_list_blood_stock_offers_kernel(
             wa_codes[:].bitcast(U16).rearrange("p (g t m) -> p g t m", g=4, t=4),
             wa_raw[:].bitcast(U16).rearrange("p (g m t) -> p g t m", g=4, t=4),
         )
-        raw["wb10"] = placed_at([P, 2048], F32, "wb_second", 0)[:]
-        load_rows(raw["wb10"], wb[512:, :512])
         first_words = held([P, S], U32, "first_words")
         nc.vector.tensor_copy(first_words[:], word_table[0][:].indirect(picks[:]))
-        late = placed_at([P, 4 * 2048 + S + 16], F32, "late", 20480)
+        late = placed_at([P, 5 * 2048 + S + 16], F32, "late", 8192)
         pieces = (
-            ("wb01", wb[:512, 512:]), ("wb11", wb[512:, 512:]),
+            ("wb10", wb[512:, :512]), ("wb01", wb[:512, 512:]), ("wb11", wb[512:, 512:]),
             ("wc0", wc[:512, :]), ("wc1", wc[512:, :]),
         )
         for n, (name, src) in enumerate(pieces):
             raw[name] = late[:, 2048 * n : 2048 * (n + 1)]
             load_rows(raw[name], src)
-        wgo_sb = late[:, 4 * 2048 : 4 * 2048 + S]
-        low_sb = late[:, 4 * 2048 + S : 4 * 2048 + S + 4]
+        wgo_sb = late[:, 5 * 2048 : 5 * 2048 + S]
+        low_sb = late[:, 5 * 2048 + S : 5 * 2048 + S + 4]
         nc.sync.dma_start(low_sb, low.rearrange("(p i) -> p i", i=4))
         nc.sync.dma_start(wgo_sb[:, :EARLY], wgo[:, :EARLY])
         nc.sync.dma_start(wgo_sb[:, EARLY:], wgo[:, EARLY:])
@@ -120,8 +119,11 @@ def tile_list_blood_stock_offers_kernel(
         nc.vector.tensor_copy(second_head[:], word_table[1][:].indirect(picks[:, : EARLY // 16]))
         second_rest = held([P, S - EARLY], U32, "second_rest")
         nc.vector.tensor_copy(second_rest[:], word_table[1][:].indirect(picks[:, EARLY // 16 :]))
-        pages.append(placed_at([P, T2], F32, "page2", 8192))
+        pages.append(placed_at([P, T2], F32, "page2", 0))
         nc.gpsimd.memset(pages[2][:], 0.0)
+        pages.append(held([P, T2], F32, "page3", tag="word_table0"))
+        nc.gpsimd.memset(pages[3][:, : T2 // 2], 0.0)
+        nc.vector.memset(pages[3][:, T2 // 2 :], 0.0)
 
         def v_words(a, col):
             if a == 0:
@@ -227,12 +229,12 @@ def tile_list_blood_stock_offers_kernel(
             )
             return dst
 
-        def weigh_on_gpsimd(y_sb, i, j0, name, raised=None):
+        def weigh_on_gpsimd(y_sb, i, j0, name, weighed=None):
             width = y_sb.shape[1]
-            if raised is None:
-                raised = own(name + "_raised", width, F32)
+            raised = own(name + "_raised", width, F32)
             nc.gpsimd.tensor_scalar(raised, y_sb, FLOAT_MAX, low_sb[:, i : i + 1], ALU.min, ALU.max)
-            weighed = own(name + "_weighed", width, F32)
+            if weighed is None:
+                weighed = own(name + "_weighed", width, F32)
             nc.gpsimd.tensor_tensor(weighed, raised, wgo_sb[:, j0 : j0 + width], ALU.mult)
             return weighed
 
@@ -283,21 +285,22 @@ def tile_list_blood_stock_offers_kernel(
         y1 = to_sbuf(y1, "y1_first")
         quantise_weight("wc1", 2, 4)
         y2 = to_sbuf(offers(y_banks[0][:], 2, spans), "y2_first")
-        y3 = offers(y_banks[2][:], 3, spans)
+        y3 = to_sbuf(offers(y_banks[2][:], 3, spans), "y3_first")
         put(0, 0, first)
         put(1, 0, weigh_on_gpsimd(y1, 1, 0, "r0s1"))
         put(2, 0, weigh_on_gpsimd(y2, 2, 0, "r0s2"))
-        pages.append(held([P, T2], F32, "page3", tag="y2_first"))
-        nc.gpsimd.memset(pages[3][:], 0.0)
         room = raw["wc1"].bitcast(BF16)
+        ends = own("ends", 192 + 256, F32)
+        last = ends[:, :256]
+        weigh_on_gpsimd(y3[:, :192], 3, 0, "r0s3", last[:, :192])
         a1 = reading("a", 1, range(2, 5), room[:, :1536])
-        a0 = reading("a", 0, range(4, 5), room[:, 3584:])
+        a0 = reading("a", 0, range(4, 5), room[:, 3072:3584])
         b1 = reading("b", 1, range(2, 5), room[:, 1536:3072])
-        b0 = reading("b", 0, range(4, 5), room[:, 3072:3584])
+        b0 = reading("b", 0, range(4, 5), ends[:, 192:].bitcast(BF16))
         h1 = lower(own("h1_mid", 1536), a1, b1)
         h0 = lower(own("h0_mid", 512), a0, b0)
         quantise_h(1, 2, h1)
-        last = weigh_from_bank(raw["wc1"][:, 1536:1792], y3, 3, 0)
+        weigh_from_bank(last[:, 192:], y3[:, 192:], 3, 192)
         quantise_h(0, 4, h0)
 
         spans = ((256, 256), (512, 128))
@@ -308,11 +311,16 @@ def tile_list_blood_stock_offers_kernel(
         first = weigh_from_bank(own("first1", 384, F32), y0, 0, 256)
         y1 = to_sbuf(y1, "y1_mid")
         y3 = to_sbuf(y3, "y3_mid")
-        y2 = offers(y_banks[0][:], 2, spans)
+        y2 = to_sbuf(offers(y_banks[0][:], 2, spans), "y2_mid")
         put(0, 256, first)
         put(1, 256, weigh_on_gpsimd(y1, 1, 256, "r1s1"))
-        room = own("end_room", 4 * 768, F32)
-        quarter = [room[:, 768 * n : 768 * (n + 1)] for n in range(4)]
+        room = own("end_room", 4 * 768 + 2 * LEAD, F32)
+        at = (0, 768, 1536 + LEAD, 2304 + 2 * LEAD)
+        quarter = [room[:, c : c + 768] for c in at]
+        values = {i: room[:, at[i] - LEAD : at[i] - LEAD + 384] for i in (2, 3)}
+        y_mid = {2: y2, 3: y3}
+        for i in (3, 2):
+            weigh_on_gpsimd(y_mid[i][:, :LEAD], i, 256, "r1s%d" % i, values[i][:, :LEAD])
         a0 = reading("a", 0, range(5, 8), quarter[0].bitcast(BF16))
         a1 = reading("a", 1, range(5, 8), quarter[2].bitcast(BF16))
         b0, b1 = quarter[1].bitcast(BF16), quarter[3].bitcast(BF16)
@@ -320,15 +328,15 @@ def tile_list_blood_stock_offers_kernel(
             for b, room_b in enumerate((b0, b1)):
                 reading("b", b, (u,), room_b[:, 512 * n : 512 * (n + 1)])
         h0 = lower(own("h0_end", 1536), a0, b0)
-        h1_end = own("h1_end", 768, F32)
-        h1 = lower(h1_end.bitcast(BF16), a1, b1)
+        h1 = lower(own("h1_end", 1536), a1, b1)
         quantise_h(0, 5, h0)
-        third = weigh_from_bank(quarter[2][:, :384], y2, 2, 256)
+        for i in (2, 3):
+            weigh_from_bank(values[i][:, LEAD:], y_mid[i][:, LEAD:], i, 256 + LEAD)
         quantise_h(1, 5, h1)
 
         spans = ((640, 128), (768, 256))
-        put(2, 256, third)
-        put(3, 256, weigh_on_gpsimd(y3, 3, 256, "r1s3", h1_end[:, :384]))
+        for i in (2, 3):
+            put(i, 256, values[i])
         for i in range(4):
             y = to_sbuf(offers(y_banks[(i + 1) % 3][:], i, spans), "y%d_end" % i)
             put(i, 640, weigh_on_gpsimd(y, i, 640, "r2s%d" % i))

@@ -100,8 +100,8 @@ def tile_list_blood_stock_offers_kernel(
             wa_codes[:].bitcast(U16).rearrange("p (g t m) -> p g t m", g=4, t=4),
             wa_raw[:].bitcast(U16).rearrange("p (g m t) -> p g t m", g=4, t=4),
         )
-        first_words = held([P, S], U32, "first_words")
-        nc.vector.tensor_copy(first_words[:], word_table[0][:].indirect(picks[:]))
+        first_head = held([P, EARLY], U32, "first_head")
+        nc.vector.tensor_copy(first_head[:], word_table[0][:].indirect(picks[:, : EARLY // 16]))
         late = placed_at([P, 5 * 2048 + S + 16], F32, "late", 8192)
         pieces = (
             ("wb10", wb[512:, :512]), ("wb01", wb[:512, 512:]), ("wb11", wb[512:, 512:]),
@@ -117,6 +117,8 @@ def tile_list_blood_stock_offers_kernel(
         nc.sync.dma_start(wgo_sb[:, EARLY:], wgo[:, EARLY:])
         second_head = held([P, EARLY], U32, "second_head")
         nc.vector.tensor_copy(second_head[:], word_table[1][:].indirect(picks[:, : EARLY // 16]))
+        first_rest = held([P, S - EARLY], U32, "first_rest")
+        nc.vector.tensor_copy(first_rest[:], word_table[0][:].indirect(picks[:, EARLY // 16 :]))
         second_rest = held([P, S - EARLY], U32, "second_rest")
         nc.vector.tensor_copy(second_rest[:], word_table[1][:].indirect(picks[:, EARLY // 16 :]))
         pages.append(placed_at([P, T2], F32, "page2", 0))
@@ -125,12 +127,10 @@ def tile_list_blood_stock_offers_kernel(
         nc.gpsimd.memset(pages[3][:, : T2 // 2], 0.0)
         nc.vector.memset(pages[3][:, T2 // 2 :], 0.0)
 
-        def v_words(a, col):
-            if a == 0:
-                return first_words[:, col : col + UNIT]
+        def v_words(a, col, width):
             if col < EARLY:
-                return second_head[:, col : col + UNIT]
-            return second_rest[:, col - EARLY : col - EARLY + UNIT]
+                return (first_head, second_head)[a][:, col : col + width]
+            return (first_rest, second_rest)[a][:, col - EARLY : col - EARLY + width]
 
         grouped, codes, scales = {}, {}, {}
         for name in raw:
@@ -161,37 +161,59 @@ def tile_list_blood_stock_offers_kernel(
         y_banks = [psum.tile([P, 512], F32, name="y_bank%d" % n) for n in range(3)]
         used = []
 
-        def reading(which, b, units, room, against=None):
-            for n, u in enumerate(units):
-                used.append(banks[len(used) % RING])
-                bank = used[-1][:].rearrange("p (t n) -> p t n", t=4)
-                col = UNIT * u
-                for t in range(4):
-                    for a in range(2):
-                        if which == "a":
-                            c = 1024 * a + 512 * b + 128 * t
-                            lhs = wa_codes[:, 2 * c : 2 * (c + 128)].bitcast(FP4X4)
-                            lhs_scale = wa_sc[:, c : c + 128]
-                        else:
-                            name = "wb%d%d" % (a, b)
-                            lhs = codes[name][:, 128 * t : 128 * (t + 1)].bitcast(FP8X4)
-                            lhs_scale = scales[name][:, 128 * t : 128 * (t + 1)]
-                        nc.tensor.matmul_mx(
-                            out=bank[:, t, :], lhsT=lhs, lhsT_scale=lhs_scale,
-                            rhs=v_words(a, col).bitcast(FP8X4),
-                            rhs_scale=v_scales[:, S * a + col : S * a + col + UNIT],
-                            start=(a == 0), stop=(a == 1),
-                        )
-                cols = slice(512 * n, 512 * (n + 1))
-                dst = room[:, cols].rearrange("p (n t) -> p n t", t=4)
-                if against is None:
-                    nc.scalar.copy(dst, bank.rearrange("p t n -> p n t"))
+        def next_bank():
+            used.append(banks[len(used) % RING])
+            return used[-1][:]
+
+        def passes(bank, which, a, b, slices, col):
+            width = 512 // len(slices)
+            for n, t in enumerate(slices):
+                if which == "a":
+                    c = 1024 * a + 512 * b + 128 * t
+                    lhs = wa_codes[:, 2 * c : 2 * (c + 128)].bitcast(FP4X4)
+                    lhs_scale = wa_sc[:, c : c + 128]
                 else:
-                    nc.vector.tensor_tensor(
-                        dst, bank.rearrange("p t n -> p n t"),
-                        against[:, cols].rearrange("p (n t) -> p n t", t=4), ALU.min,
-                    )
+                    name = "wb%d%d" % (a, b)
+                    lhs = codes[name][:, 128 * t : 128 * (t + 1)].bitcast(FP8X4)
+                    lhs_scale = scales[name][:, 128 * t : 128 * (t + 1)]
+                nc.tensor.matmul_mx(
+                    out=bank[:, width * n : width * (n + 1)], lhsT=lhs, lhsT_scale=lhs_scale,
+                    rhs=v_words(a, col, width).bitcast(FP8X4),
+                    rhs_scale=v_scales[:, S * a + col : S * a + col + width],
+                    start=(a, n) == (0, 0), stop=(a, n) == (1, len(slices) - 1),
+                )
+
+        def woven(room):
+            return room.rearrange("p (u n e) -> p n u e", u=2, e=2)
+
+        def by_entry(bank):
+            return bank.rearrange("p (u e n) -> p n u e", u=2, e=2)
+
+        def empty_pair(bank, room, u, at):
+            nc.scalar.copy(woven(room)[:, at : at + 2 * UNIT, u, :], bank.rearrange("p (e n) -> p n e", e=2))
+
+        def read_two(which, b, unit, room, at=0):
+            for u in range(2):
+                bank = next_bank()
+                for a in range(2):
+                    passes(bank, which, a, b, (2 * u, 2 * u + 1), UNIT * unit)
+                empty_pair(bank, room, u, at)
             return room
+
+        def read_plain(which, b, units, room):
+            for n, u in enumerate(units):
+                bank = next_bank()
+                for a in range(2):
+                    passes(bank, which, a, b, range(4), UNIT * u)
+                nc.scalar.copy(
+                    room[:, 512 * n : 512 * (n + 1)].rearrange("p (n t) -> p n t", t=4),
+                    bank.rearrange("p (t n) -> p n t", t=4),
+                )
+            return room
+
+        def lower_plain(h_bf, from_a, from_b):
+            nc.vector.tensor_tensor(h_bf, from_a, from_b, ALU.min)
+            return h_bf
 
         def own(name, columns, dtype=BF16):
             return held([P, columns], dtype, name)[:]
@@ -200,7 +222,9 @@ def tile_list_blood_stock_offers_kernel(
         h_scales = [own("h_scales%d" % b, S, U8) for b in range(2)]
 
         def lower(h_bf, from_a, from_b):
-            nc.vector.tensor_tensor(h_bf, from_a, from_b, ALU.min)
+            nc.vector.tensor_tensor(
+                h_bf.rearrange("p (n u e) -> p n u e", u=2, e=2), woven(from_a), woven(from_b), ALU.min
+            )
             return h_bf
 
         def quantise_h(b, first, h_bf):
@@ -254,20 +278,35 @@ def tile_list_blood_stock_offers_kernel(
         round_weight(nc.vector.tensor_copy, "wb00", 0, 4, slice(64, P))
         quantise_weight("wb00", 0, 4)
         weight_on_vector("wb10")
-        a0_lo = reading("a", 0, range(2), own("a0_lo", 1024))
-        a0_hi = reading("a", 0, range(2, 4), own("a0_hi", 1024))
-        a1 = reading("a", 1, range(2), own("a1", 1024))
+        a0_lo = read_two("a", 0, 0, own("a0_lo", 1024))
+        a1 = read_two("a", 1, 0, own("a1", 1024))
+        a0_hi = read_two("a", 0, 2, own("a0_hi", 1024))
         weight_on_vector("wb01")
-        b0 = reading("b", 0, range(4), own("b0", 2048))
+        b0 = own("b0", 2048)
+        opened = [(n, u, next_bank()) for n in range(2) for u in range(2)]
+        for n, u, bank in opened:
+            passes(bank, "b", 0, 0, (2 * u, 2 * u + 1), 2 * UNIT * n)
+        for n, u, bank in opened:
+            passes(bank, "b", 1, 0, (2 * u, 2 * u + 1), 2 * UNIT * n)
+            empty_pair(bank, b0[:, 1024 * n : 1024 * (n + 1)], u, 0)
         round_weight(nc.vector.tensor_copy, "wb11", 0, 4, slice(0, 88))
         round_weight(nc.scalar.copy, "wb11", 0, 4, slice(88, P))
-        h_bf = raw["wb01"][:, :1024].bitcast(BF16)
+        h_bf = late[:, 2 * 2048 - 512 : 2 * 2048 + 512].bitcast(BF16)
         lower(h_bf[:, :1024], a0_lo, b0[:, :1024])
         quantise_weight("wb11", 0, 4)
         lower(h_bf[:, 1024:], a0_hi, b0[:, 1024:])
         grouped["wc0"] = held([P, 2048], BF16, "wc0_bf", tag="a0_lo")[:]
         round_weight(nc.scalar.copy, "wc0", 0, 2)
-        h1_bf = reading("b", 1, range(2), raw["wb11"][:, 1024:1536].bitcast(BF16), a1)
+        h1_bf = raw["wb11"][:, 1024:1536].bitcast(BF16)
+        singles = [next_bank() for u in range(2)]
+        for a in range(2):
+            for u in range(2):
+                passes(singles[u], "b", a, 1, range(4), UNIT * u)
+        for u in range(2):
+            nc.vector.tensor_tensor(
+                h1_bf[:, 512 * u : 512 * (u + 1)].rearrange("p (n u e) -> p n u e", u=2, e=2),
+                by_entry(singles[u]), woven(a1)[:, UNIT * u : UNIT * (u + 1)], ALU.min,
+            )
         quantise_h(0, 0, h_bf)
         quantise_h(1, 0, h1_bf)
         quantise_weight("wc0", 0, 2)
@@ -293,12 +332,12 @@ def tile_list_blood_stock_offers_kernel(
         ends = own("ends", 192 + 256, F32)
         last = ends[:, :256]
         weigh_on_gpsimd(y3[:, :192], 3, 0, "r0s3", last[:, :192])
-        a1 = reading("a", 1, range(2, 5), room[:, :1536])
-        a0 = reading("a", 0, range(4, 5), room[:, 3072:3584])
-        b1 = reading("b", 1, range(2, 5), room[:, 1536:3072])
-        b0 = reading("b", 0, range(4, 5), ends[:, 192:].bitcast(BF16))
-        h1 = lower(own("h1_mid", 1536), a1, b1)
-        h0 = lower(own("h0_mid", 512), a0, b0)
+        a1 = read_plain("a", 1, range(2, 5), room[:, :1536])
+        a0 = read_plain("a", 0, range(4, 5), room[:, 3072:3584])
+        b1 = read_plain("b", 1, range(2, 5), room[:, 1536:3072])
+        b0 = read_plain("b", 0, range(4, 5), ends[:, 192:].bitcast(BF16))
+        h1 = lower_plain(own("h1_mid", 1536), a1, b1)
+        h0 = lower_plain(own("h0_mid", 512), a0, b0)
         quantise_h(1, 2, h1)
         weigh_from_bank(last[:, 192:], y3[:, 192:], 3, 192)
         quantise_h(0, 4, h0)
@@ -321,14 +360,14 @@ def tile_list_blood_stock_offers_kernel(
         y_mid = {2: y2, 3: y3}
         for i in (3, 2):
             weigh_on_gpsimd(y_mid[i][:, :LEAD], i, 256, "r1s%d" % i, values[i][:, :LEAD])
-        a0 = reading("a", 0, range(5, 8), quarter[0].bitcast(BF16))
-        a1 = reading("a", 1, range(5, 8), quarter[2].bitcast(BF16))
-        b0, b1 = quarter[1].bitcast(BF16), quarter[3].bitcast(BF16)
+        a0, b0, a1, b1 = [part.bitcast(BF16) for part in quarter]
+        for b, room_a in enumerate((a0, a1)):
+            read_plain("a", b, range(5, 8), room_a)
         for n, u in enumerate(range(5, 8)):
             for b, room_b in enumerate((b0, b1)):
-                reading("b", b, (u,), room_b[:, 512 * n : 512 * (n + 1)])
-        h0 = lower(own("h0_end", 1536), a0, b0)
-        h1 = lower(own("h1_end", 1536), a1, b1)
+                read_plain("b", b, (u,), room_b[:, 512 * n : 512 * (n + 1)])
+        h0 = lower_plain(own("h0_end", 1536), a0, b0)
+        h1 = lower_plain(own("h1_end", 1536), a1, b1)
         quantise_h(0, 5, h0)
         for i in (2, 3):
             weigh_from_bank(values[i][:, LEAD:], y_mid[i][:, LEAD:], i, 256 + LEAD)

from contextlib import ExitStack

import concourse.mybir as mybir

K, H, N, T, S, T2 = 1024, 1024, 512, 2048, 1024, 2048
FLOPS = 2 * (2 * K * H * S + H * N * S)

F32 = mybir.dt.float32
BF16 = mybir.dt.bfloat16
I32 = mybir.dt.int32
U32 = mybir.dt.uint32
U16 = mybir.dt.uint16
U8 = mybir.dt.uint8
FP8X4 = mybir.dt.float8_e4m3fn_x4
FP4X4 = mybir.dt.float4_e2m1fn_x4
ALU = mybir.AluOpType

P = 128
UNIT = 128
RING = 5
EARLY = 256
LEAD = 320
FLOAT_MAX = 3.4028234663852886e38


def tile_list_blood_stock_offers_kernel(
    tc, tab_words, tab_scales, offs, wa_words, wa_scales, wb, wc, low, wgo, offs2, out
):
    nc = tc.nc
    with ExitStack() as ctx:
        keep = ctx.enter_context(tc.tile_pool(name="keep", bufs=1))
        laid = ctx.enter_context(tc.tile_pool(name="laid", bufs=1))
        psum = ctx.enter_context(tc.psum_pool(name="psum", bufs=1))

        def held(shape, dtype, name, tag=None):
            return keep.tile(shape, dtype, name=name, tag=tag or name, align_bytes=64)

        def placed_at(shape, dtype, name, offset):
            return laid.tile(shape, dtype, name=name, tag=name, align_bytes=64, offset=offset)

        picks = keep.tile([P, S // 16], U16, name="picks")
        nc.sync.dma_start(picks[:], offs)
        wa_raw = held([P, 4096], U8, "wa_raw")
        nc.sync.dma_start(
            wa_raw[:].bitcast(I32).rearrange("p (a n) -> p a n", a=2),
            wa_words.bitcast(I32).rearrange("a p n -> p a n"),
        )
        slots = keep.tile([P, S // 16], U16, name="slots")
        nc.sync.dma_start(slots[:], offs2)
        scale_table = held([P, T], U8, "scale_table")
        nc.vector.memset(scale_table[:].bitcast(I32), 0)
        nc.sync.dma_start(
            scale_table[0:P:4, :].bitcast(I32), tab_scales.bitcast(I32).rearrange("a q n -> q a n")
        )
        word_table = [held([P, T], U32, "word_table%d" % a) for a in range(2)]

        def load_words(a):
            nc.sync.dma_start(
                word_table[a][:].bitcast(I32), tab_words[a].rearrange("p n t -> p (n t)").bitcast(I32)
            )

        load_words(0)
        load_words(1)
        was_raw = placed_at([P, 2048], U8, "was_raw", 7168)
        nc.gpsimd.memset(was_raw[:].bitcast(I32), 0)
        was_rows = wa_scales.bitcast(I32).rearrange("a (d r) n -> r d a n", r=4)
        for r in range(4):
            nc.scalar.dma_start(
                was_raw[r:P:32, :].bitcast(I32).rearrange("p (a n) -> p a n", a=2), was_rows[r]
            )

        def load_rows(dst, src):
            nc.sync.dma_start(dst.rearrange("p (j c) -> p j c", j=4), src.rearrange("(p j) c -> p j c", j=4))

        wb_first = held([P, 2048], F32, "wb_first")
        raw = {"wb00": wb_first[:]}
        load_rows(raw["wb00"], wb[0:512, 0:512])

        v_scales = held([P, 2 * S], U8, "v_scales")
        nc.vector.memset(v_scales[:].bitcast(I32), 0)
        pages = [held([P, T2], F32, "page%d" % i) for i in range(2)]
        for i in range(2):
            nc.vector.memset(pages[i][:], 0.0)

        picked_scales = held([P, S], U8, "picked_scales")
        nc.vector.tensor_copy(picked_scales[:], scale_table[:].indirect(picks[:]))
        for d in range(4):
            nc.scalar.dma_start(
                v_scales[32 * d : 32 * d + 4, :].bitcast(I32),
                picked_scales[32 * d : 32 * (d + 1) : 4, :].bitcast(I32),
            )

        wa_sc = held([P, 2048], U8, "wa_sc", tag="scale_table")
        nc.vector.tensor_copy(
            wa_sc[:].rearrange("p (g t m) -> p g t m", g=4, t=4),
            was_raw[:].rearrange("p (g m t) -> p g t m", g=4, t=4),
        )
        wa_codes = held([P, 4096], U8, "wa_codes")
        nc.scalar.copy(
            wa_codes[:].bitcast(U16).rearrange("p (g t m) -> p g t m", g=4, t=4),
            wa_raw[:].bitcast(U16).rearrange("p (g m t) -> p g t m", g=4, t=4),
        )
        first_head = held([P, EARLY], U32, "first_head")
        nc.vector.tensor_copy(first_head[:], word_table[0][:].indirect(picks[:, : EARLY // 16]))
        late = placed_at([P, 5 * 2048 + S + 16], F32, "late", 8192)
        pieces = (
            ("wb10", wb[512:, :512]), ("wb01", wb[:512, 512:]), ("wb11", wb[512:, 512:]),
            ("wc0", wc[:512, :]), ("wc1", wc[512:, :]),
        )
        for n, (name, src) in enumerate(pieces):
            raw[name] = late[:, 2048 * n : 2048 * (n + 1)]
            load_rows(raw[name], src)
        wgo_sb = late[:, 5 * 2048 : 5 * 2048 + S]
        low_sb = late[:, 5 * 2048 + S : 5 * 2048 + S + 4]
        nc.sync.dma_start(low_sb, low.rearrange("(p i) -> p i", i=4))
        nc.sync.dma_start(wgo_sb[:, :EARLY], wgo[:, :EARLY])
        nc.sync.dma_start(wgo_sb[:, EARLY:], wgo[:, EARLY:])
        second_head = held([P, EARLY], U32, "second_head")
        nc.vector.tensor_copy(second_head[:], word_table[1][:].indirect(picks[:, : EARLY // 16]))
        first_rest = held([P, S - EARLY], U32, "first_rest")
        nc.vector.tensor_copy(first_rest[:], word_table[0][:].indirect(picks[:, EARLY // 16 :]))
        second_rest = held([P, S - EARLY], U32, "second_rest")
        nc.vector.tensor_copy(second_rest[:], word_table[1][:].indirect(picks[:, EARLY // 16 :]))
        pages.append(placed_at([P, T2], F32, "page2", 0))
        nc.gpsimd.memset(pages[2][:], 0.0)
        pages.append(held([P, T2], F32, "page3", tag="word_table0"))
        nc.gpsimd.memset(pages[3][:, : T2 // 2], 0.0)
        nc.vector.memset(pages[3][:, T2 // 2 :], 0.0)

        def v_words(a, col, width):
            if col < EARLY:
                return (first_head, second_head)[a][:, col : col + width]
            return (first_rest, second_rest)[a][:, col - EARLY : col - EARLY + width]

        grouped, codes, scales = {}, {}, {}
        for name in raw:
            if name.startswith("wb"):
                grouped[name] = held([P, 2048], BF16, name + "_bf")[:]
            codes[name] = held([P, 512], U32, name + "_codes")[:]
            scales[name] = held([P, 512], U8, name + "_scales")[:]

        def round_weight(copy, name, lo, hi, rows=slice(0, P)):
            src = raw[name].rearrange("p (j m t) -> p m j t", j=4, t=4)
            dst = grouped[name].rearrange("p (t m j) -> p m j t", t=4, j=4)
            copy(dst[:, rows, :, lo:hi], src[:, rows, :, lo:hi])

        def quantise(to_codes, to_scales, values):
            nc.vector.quantize_mx(out=to_codes.bitcast(FP8X4), scales=to_scales, in_=values)

        def quantise_weight(name, lo, hi):
            quantise(
                codes[name][:, P * lo : P * hi], scales[name][:, P * lo : P * hi],
                grouped[name][:, 512 * lo : 512 * hi],
            )

        def weight_on_vector(name):
            round_weight(nc.vector.tensor_copy, name, 0, 4)
            quantise_weight(name, 0, 4)

        banks = [psum.tile([P, 512], F32, name="bank%d" % n) for n in range(RING)]
        y_banks = [psum.tile([P, 512], F32, name="y_bank%d" % n) for n in range(3)]
        used = []

        def next_bank():
            used.append(banks[len(used) % RING])
            return used[-1][:]

        def passes(bank, which, a, b, slices, col):
            width = 512 // len(slices)
            for n, t in enumerate(slices):
                if which == "a":
                    c = 1024 * a + 512 * b + 128 * t
                    lhs = wa_codes[:, 2 * c : 2 * (c + 128)].bitcast(FP4X4)
                    lhs_scale = wa_sc[:, c : c + 128]
                else:
                    name = "wb%d%d" % (a, b)
                    lhs = codes[name][:, 128 * t : 128 * (t + 1)].bitcast(FP8X4)
                    lhs_scale = scales[name][:, 128 * t : 128 * (t + 1)]
                nc.tensor.matmul_mx(
                    out=bank[:, width * n : width * (n + 1)], lhsT=lhs, lhsT_scale=lhs_scale,
                    rhs=v_words(a, col, width).bitcast(FP8X4),
                    rhs_scale=v_scales[:, S * a + col : S * a + col + width],
                    start=(a, n) == (0, 0), stop=(a, n) == (1, len(slices) - 1),
                )

        def woven(room):
            return room.rearrange("p (u n e) -> p n u e", u=2, e=2)

        def by_entry(bank):
            return bank.rearrange("p (u e n) -> p n u e", u=2, e=2)

        def empty_pair(bank, room, u, at):
            nc.scalar.copy(woven(room)[:, at : at + 2 * UNIT, u, :], bank.rearrange("p (e n) -> p n e", e=2))

        def read_two(which, b, unit, room, at=0):
            for u in range(2):
                bank = next_bank()
                for a in range(2):
                    passes(bank, which, a, b, (2 * u, 2 * u + 1), UNIT * unit)
                empty_pair(bank, room, u, at)
            return room

        def read_plain(which, b, units, room):
            for n, u in enumerate(units):
                bank = next_bank()
                for a in range(2):
                    passes(bank, which, a, b, range(4), UNIT * u)
                nc.scalar.copy(
                    room[:, 512 * n : 512 * (n + 1)].rearrange("p (n t) -> p n t", t=4),
                    bank.rearrange("p (t n) -> p n t", t=4),
                )
            return room

        def lower_plain(h_bf, from_a, from_b):
            nc.vector.tensor_tensor(h_bf, from_a, from_b, ALU.min)
            return h_bf

        def own(name, columns, dtype=BF16):
            return held([P, columns], dtype, name)[:]

        h_codes = [own("h_codes%d" % b, S, U32) for b in range(2)]
        h_scales = [own("h_scales%d" % b, S, U8) for b in range(2)]

        def lower(h_bf, from_a, from_b):
            nc.vector.tensor_tensor(
                h_bf.rearrange("p (n u e) -> p n u e", u=2, e=2), woven(from_a), woven(from_b), ALU.min
            )
            return h_bf

        def quantise_h(b, first, h_bf):
            cols = slice(UNIT * first, UNIT * first + h_bf.shape[1] // 4)
            quantise(h_codes[b][:, cols], h_scales[b][:, cols], h_bf)

        def offers(bank, i, spans):
            at = 0
            for j0, width in spans:
                for b in range(2):
                    name = "wc%d" % b
                    nc.tensor.matmul_mx(
                        out=bank[:, at : at + width],
                        lhsT=codes[name][:, 128 * i : 128 * (i + 1)].bitcast(FP8X4),
                        lhsT_scale=scales[name][:, 128 * i : 128 * (i + 1)],
                        rhs=h_codes[b][:, j0 : j0 + width].bitcast(FP8X4),
                        rhs_scale=h_scales[b][:, j0 : j0 + width],
                        start=(b == 0), stop=(b == 1),
                    )
                at += width
            return bank[:, :at]

        def weigh_from_bank(dst, y, i, j0):
            nc.vector.scalar_tensor_tensor(
                dst, y, low_sb[:, i : i + 1], wgo_sb[:, j0 : j0 + y.shape[1]], ALU.max, ALU.mult
            )
            return dst

        def weigh_on_gpsimd(y_sb, i, j0, name, weighed=None):
            width = y_sb.shape[1]
            raised = own(name + "_raised", width, F32)
            nc.gpsimd.tensor_scalar(raised, y_sb, FLOAT_MAX, low_sb[:, i : i + 1], ALU.min, ALU.max)
            if weighed is None:
                weighed = own(name + "_weighed", width, F32)
            nc.gpsimd.tensor_tensor(weighed, raised, wgo_sb[:, j0 : j0 + width], ALU.mult)
            return weighed

        def to_sbuf(y, name):
            y_sb = own(name, y.shape[1], F32)
            nc.scalar.copy(y_sb, y)
            return y_sb

        out_rows = out.rearrange("(p i) n -> i p n", i=4)

        def put(i, j0, values):
            nc.vector.tensor_copy(
                pages[i][:].indirect(slots[:, j0 // 16 : (j0 + values.shape[1]) // 16]), values
            )

        round_weight(nc.scalar.copy, "wb00", 0, 4, slice(0, 64))
        round_weight(nc.vector.tensor_copy, "wb00", 0, 4, slice(64, P))
        quantise_weight("wb00", 0, 4)
        weight_on_vector("wb10")
        a0_lo = read_two("a", 0, 0, own("a0_lo", 1024))
        a1 = read_two("a", 1, 0, own("a1", 1024))
        a0_hi = read_two("a", 0, 2, own("a0_hi", 1024))
        weight_on_vector("wb01")
        b0 = own("b0", 2048)
        opened = [(n, u, next_bank()) for n in range(2) for u in range(2)]
        for n, u, bank in opened:
            passes(bank, "b", 0, 0, (2 * u, 2 * u + 1), 2 * UNIT * n)
        for n, u, bank in opened:
            passes(bank, "b", 1, 0, (2 * u, 2 * u + 1), 2 * UNIT * n)
            empty_pair(bank, b0[:, 1024 * n : 1024 * (n + 1)], u, 0)
        round_weight(nc.vector.tensor_copy, "wb11", 0, 4, slice(0, 88))
        round_weight(nc.scalar.copy, "wb11", 0, 4, slice(88, P))
        h_bf = late[:, 2 * 2048 - 512 : 2 * 2048 + 512].bitcast(BF16)
        lower(h_bf[:, :1024], a0_lo, b0[:, :1024])
        quantise_weight("wb11", 0, 4)
        lower(h_bf[:, 1024:], a0_hi, b0[:, 1024:])
        grouped["wc0"] = held([P, 2048], BF16, "wc0_bf", tag="a0_lo")[:]
        round_weight(nc.scalar.copy, "wc0", 0, 2)
        h1_bf = raw["wb11"][:, 1024:1536].bitcast(BF16)
        singles = [next_bank() for u in range(2)]
        for a in range(2):
            for u in range(2):
                passes(singles[u], "b", a, 1, range(4), UNIT * u)
        for u in range(2):
            nc.vector.tensor_tensor(
                h1_bf[:, 512 * u : 512 * (u + 1)].rearrange("p (n u e) -> p n u e", u=2, e=2),
                by_entry(singles[u]), woven(a1)[:, UNIT * u : UNIT * (u + 1)], ALU.min,
            )
        quantise_h(0, 0, h_bf)
        quantise_h(1, 0, h1_bf)
        quantise_weight("wc0", 0, 2)
        round_weight(nc.scalar.copy, "wc0", 2, 4)
        grouped["wc1"] = held([P, 2048], BF16, "wc1_bf", tag="a0_hi")[:]
        round_weight(nc.scalar.copy, "wc1", 0, 2)
        round_weight(nc.scalar.copy, "wc1", 2, 4)
        quantise_weight("wc1", 0, 2)
        quantise_weight("wc0", 2, 4)

        spans = ((0, 256),)
        y0 = offers(y_banks[0][:], 0, spans)
        y1 = offers(y_banks[1][:], 1, spans)
        first = weigh_from_bank(own("first", 256, F32), y0, 0, 0)
        y1 = to_sbuf(y1, "y1_first")
        quantise_weight("wc1", 2, 4)
        y2 = to_sbuf(offers(y_banks[0][:], 2, spans), "y2_first")
        y3 = to_sbuf(offers(y_banks[2][:], 3, spans), "y3_first")
        put(0, 0, first)
        put(1, 0, weigh_on_gpsimd(y1, 1, 0, "r0s1"))
        put(2, 0, weigh_on_gpsimd(y2, 2, 0, "r0s2"))
        room = raw["wc1"].bitcast(BF16)
        ends = own("ends", 192 + 256, F32)
        last = ends[:, :256]
        weigh_on_gpsimd(y3[:, :192], 3, 0, "r0s3", last[:, :192])
        a1 = read_plain("a", 1, range(2, 5), room[:, :1536])
        a0 = read_plain("a", 0, range(4, 5), room[:, 3072:3584])
        b1 = read_plain("b", 1, range(2, 5), room[:, 1536:3072])
        b0 = read_plain("b", 0, range(4, 5), ends[:, 192:].bitcast(BF16))
        h1 = lower_plain(own("h1_mid", 1536), a1, b1)
        h0 = lower_plain(own("h0_mid", 512), a0, b0)
        quantise_h(1, 2, h1)
        weigh_from_bank(last[:, 192:], y3[:, 192:], 3, 192)
        quantise_h(0, 4, h0)

        spans = ((256, 256), (512, 128))
        y0 = offers(y_banks[0][:], 0, spans)
        y1 = offers(y_banks[1][:], 1, spans)
        y3 = offers(y_banks[2][:], 3, spans)
        put(3, 0, last)
        first = weigh_from_bank(own("first1", 384, F32), y0, 0, 256)
        y1 = to_sbuf(y1, "y1_mid")
        y3 = to_sbuf(y3, "y3_mid")
        y2 = to_sbuf(offers(y_banks[0][:], 2, spans), "y2_mid")
        put(0, 256, first)
        put(1, 256, weigh_on_gpsimd(y1, 1, 256, "r1s1"))
        room = own("end_room", 4 * 768 + 2 * LEAD, F32)
        at = (0, 768, 1536 + LEAD, 2304 + 2 * LEAD)
        quarter = [room[:, c : c + 768] for c in at]
        values = {i: room[:, at[i] - LEAD : at[i] - LEAD + 384] for i in (2, 3)}
        y_mid = {2: y2, 3: y3}
        for i in (3, 2):
            weigh_on_gpsimd(y_mid[i][:, :LEAD], i, 256, "r1s%d" % i, values[i][:, :LEAD])
        a0, b0, a1, b1 = [part.bitcast(BF16) for part in quarter]
        for b, room_a in enumerate((a0, a1)):
            read_plain("a", b, range(5, 8), room_a)
        for n, u in enumerate(range(5, 8)):
            for b, room_b in enumerate((b0, b1)):
                read_plain("b", b, (u,), room_b[:, 512 * n : 512 * (n + 1)])
        h0 = lower_plain(own("h0_end", 1536), a0, b0)
        h1 = lower_plain(own("h1_end", 1536), a1, b1)
        quantise_h(0, 5, h0)
        for i in (2, 3):
            weigh_from_bank(values[i][:, LEAD:], y_mid[i][:, LEAD:], i, 256 + LEAD)
        quantise_h(1, 5, h1)

        spans = ((640, 128), (768, 256))
        for i in (2, 3):
            put(i, 256, values[i])
        for i in range(4):
            y = to_sbuf(offers(y_banks[(i + 1) % 3][:], i, spans), "y%d_end" % i)
            put(i, 640, weigh_on_gpsimd(y, i, 640, "r2s%d" % i))
            nc.sync.dma_start(out_rows[i], pages[i][:])
